import numpy as np
import ml_dtypes


def mxq(x, axis, fmt="e4m3"):
    dtype, down = {"e4m3": (ml_dtypes.float8_e4m3fn, 7), "e5m2": (ml_dtypes.float8_e5m2, 14)}[fmt]
    v = np.moveaxis(np.asarray(x, np.float32).astype(ml_dtypes.bfloat16).astype(np.float64), axis, -1)
    blocks = v.reshape(v.shape[:-1] + (-1, 32))
    amax = np.abs(blocks).max(-1, keepdims=True)
    byte = np.maximum(np.where(amax > 0, np.frexp(amax)[1] - 1 + 127, 0) - down, 1)
    scale = np.exp2(byte - 127.0)
    codes = (blocks / scale).astype(np.float32).astype(dtype).astype(np.float64)
    return np.moveaxis((codes * scale).reshape(v.shape), -1, axis)


WIDE = False


def mx_kscale(k):
    if not WIDE:
        return np.ones(k)
    levels = np.array([10, -10, 5, -5, 0])
    if k % 512:
        return np.exp2(np.random.permutation(np.resize(levels, k // 32))).repeat(32)
    a = np.empty((k // 512, 16))
    for p in range(k // 512):
        a[p, :8] = np.random.permutation(np.resize(levels, 8))
        for g in range(8):
            far = levels[np.abs(levels - a[p, g]) >= 10]
            a[p, g + 8] = far[np.random.randint(len(far))]
    return np.exp2(a.ravel()).repeat(32)


def f64(x):
    return np.asarray(x).astype(np.float64)


def striped(idx):
    return np.tile(idx.reshape(-1, 16).T, (8, 1)).astype(np.uint16)


def unstriped(offs):
    return offs[:16].T.reshape(-1).astype(np.int64)


def pack_weight(w):
    k, n = w.shape
    w = f64(np.asarray(w, np.float32).astype(ml_dtypes.bfloat16)).reshape(k // 32, 32, n)
    amax = np.abs(w).max(1)
    byte = np.clip(np.where(amax > 0, np.frexp(amax)[1] - 1 + 127 - 7, 1), 1, 254)
    scaled = (w * np.exp2(127.0 - byte)[:, None, :]).reshape(k, n).astype(np.float32)
    words = np.ascontiguousarray(scaled.reshape(k // 512, 128, 4, n).transpose(0, 1, 3, 2)).astype(ml_dtypes.float8_e4m3fn).view(np.uint8)
    return words, np.ascontiguousarray(byte.astype(np.uint8).reshape(k // 512, 16, n))


def unpack_weight(words, scales):
    g, p, n, _ = words.shape
    vals = np.ascontiguousarray(words).view(ml_dtypes.float8_e4m3fn).astype(np.float64) * np.repeat(np.exp2(scales.astype(np.float64) - 127.0), 8, axis=1)[..., None]
    return vals.transpose(0, 1, 3, 2).reshape(g * 512, n)


def relu(v):
    return np.maximum(v, 0.0)


K, T, S, D, V, N = 512, 2048, 1024, 2, 512, 256
P = 2 ** 7


def setup_inputs():
    n = np.random.standard_normal
    s = mx_kscale(K)[:, None]
    packed_xT = pack_weight(n((K, T)) * s)
    return {
        "x_words": packed_xT[0],
        "x_scales": packed_xT[1],
        "w1": (n((K, N)) / np.sqrt(K) / s).astype(np.float32),
        "gate": (np.tile(np.random.uniform(0.2, 1.0, (D, 1, V)) / np.sqrt(D), (1, P, 1))).astype(np.float32),
        "offs": striped(np.random.permutation(T)[:S]),
        "cen": striped(np.random.permutation(S)[:V]),
        "pos1": striped(np.random.permutation(S)[:V]),
        "pos2": striped(np.random.permutation(S)[:V]),
    }


def reference(x_words, x_scales, w1, gate, offs, cen, pos1, pos2):
    xq = unpack_weight(x_words, x_scales)[:, unstriped(offs)]
    y = relu(mxq(f64(w1), 0, "e4m3").T @ xq)
    yc = y[:, unstriped(cen)]
    return yc + (y[:, unstriped(pos1)] - yc) * f64(gate)[0, :1] + (y[:, unstriped(pos2)] - yc) * f64(gate)[1, :1]

@@ -1,0 +1,137 @@
+from contextlib import ExitStack
+
+import concourse.mybir as mybir
+from concourse.masks import make_identity
+
+K, T, S, V, N = 512, 2048, 1024, 512, 256
+FLOPS = 2 * K * N * S
+
+F32 = mybir.dt.float32
+BF16 = mybir.dt.bfloat16
+I32 = mybir.dt.int32
+U32 = mybir.dt.uint32
+U16 = mybir.dt.uint16
+U8 = mybir.dt.uint8
+FP8X4 = mybir.dt.float8_e4m3fn_x4
+ALU = mybir.AluOpType
+ACT = mybir.ActivationFunctionType
+
+P = 128
+PACK = 4
+LANES = 16
+QUAD = 32
+BANK = 512
+CHUNK = 256
+
+
+def tile_picked_grand_relu_p_kernel(tc, x_words, x_scales, w1, gate, offs, cen, pos1, pos2, out):
+    nc = tc.nc
+    with ExitStack() as ctx:
+        keep = ctx.enter_context(tc.tile_pool(name="keep", bufs=1))
+        work = ctx.enter_context(tc.tile_pool(name="work", bufs=2))
+        psum = ctx.enter_context(tc.psum_pool(name="psum", bufs=1))
+        turn = ctx.enter_context(tc.psum_pool(name="turn", bufs=2))
+
+        offs_t = keep.tile([P, S // LANES], U16, name="offs_t")
+        cen_t = keep.tile([P, V // LANES], U16, name="cen_t")
+        pos1_t = keep.tile([P, V // LANES], U16, name="pos1_t")
+        pos2_t = keep.tile([P, V // LANES], U16, name="pos2_t")
+        scale_tab = keep.tile([P, T], U8, name="scale_tab", align_bytes=64)
+        word_tab = keep.tile([P, T], I32, name="word_tab", align_bytes=64)
+        w_raw = keep.tile([P, PACK, N], F32, name="w_raw")
+        gate_t = keep.tile([P, 2, V], F32, name="gate_t")
+
+        nc.sync.dma_start(offs_t[:], offs)
+        for q in range(P // QUAD):
+            rows = x_scales[0, PACK * q : PACK * (q + 1), :].bitcast(I32)
+            nc.sync.dma_start(
+                scale_tab[QUAD * q : QUAD * (q + 1), :].bitcast(I32),
+                rows.unsqueeze(0).broadcast_to([QUAD // PACK, PACK, T // 4]),
+            )
+        nc.sync.dma_start(word_tab[:], x_words[0].rearrange("p n t -> p (n t)").bitcast(I32))
+        nc.sync.dma_start(w_raw[:], w1.rearrange("(p j) m -> p j m", j=PACK))
+        nc.sync.dma_start(gate_t[:], gate.rearrange("d p v -> p d v"))
+        nc.sync.dma_start(pos1_t[:], pos1)
+        nc.sync.dma_start(pos2_t[:], pos2)
+        nc.sync.dma_start(cen_t[:], cen)
+
+        ident = keep.tile([P, P], F32, name="ident")
+        make_identity(nc, ident[:])
+
+        x_scale = keep.tile([P, S], U8, name="x_scale", align_bytes=64)
+        nc.vector.tensor_copy(x_scale[:], scale_tab[:].indirect(offs_t[:]))
+
+        w_codes, w_scale = [], []
+        for b in range(N // P):
+            grouped = keep.tile([P, P, PACK], BF16, name=f"grouped{b}", align_bytes=64)
+            nc.scalar.copy(grouped[:], w_raw[:, :, b * P : (b + 1) * P].rearrange("p j m -> p m j"))
+            w_codes.append(keep.tile([P, P], U32, name=f"w_codes{b}", align_bytes=64))
+            w_scale.append(keep.tile([P, P], U8, name=f"w_scale{b}", align_bytes=64))
+            nc.vector.quantize_mx(
+                out=w_codes[b][:].bitcast(FP8X4),
+                scales=w_scale[b][:],
+                in_=grouped[:].rearrange("p m j -> p (m j)"),
+            )
+
+        x_codes = keep.tile([P, S], U32, name="x_codes", align_bytes=64)
+        pieces = [(0, 512), (512, 768), (768, 1024)]
+        for a, z in pieces:
+            nc.vector.tensor_copy(
+                x_codes[:, a:z], word_tab[:].bitcast(U32).indirect(offs_t[:, a // LANES : z // LANES])
+            )
+
+        keepc = keep.tile([P, V], F32, name="keepc")
+        one_less = keep.tile([P, V], F32, name="one_less")
+        nc.scalar.activation(one_less[:], gate_t[:, 0, :], ACT.Copy, bias=1.0, scale=-1.0)
+
+        y = []
+        for b in range(N // P):
+            y.append(keep.tile([P, S], F32, name=f"y{b}"))
+            for i, (a, z) in enumerate(pieces if b == 0 else [(0, 512), (512, 1024)]):
+                acc = psum.tile([P, z - a], F32, name=f"acc{b}_{i}", tag=f"acc{(3 * b + i) % 4}")
+                nc.tensor.matmul_mx(
+                    out=acc[:],
+                    lhsT=w_codes[b][:].bitcast(FP8X4),
+                    lhsT_scale=w_scale[b][:],
+                    rhs=x_codes[:, a:z].bitcast(FP8X4),
+                    rhs_scale=x_scale[:, a:z],
+                    start=True,
+                    stop=True,
+                )
+                nc.scalar.activation(y[b][:, a:z], acc[:], ACT.Relu)
+
+        nc.vector.tensor_tensor(keepc[:], one_less[:], gate_t[:, 1, :], ALU.subtract)
+
+        terms = [(pos1_t, gate_t[:, 0, :]), (pos2_t, gate_t[:, 1, :]), (cen_t, keepc[:])]
+        chunks = [(b, v0) for b in range(N // P) for v0 in range(0, V, CHUNK)]
+        for b, v0 in chunks:
+            parts = []
+            for t, (lst, fac) in enumerate(terms):
+                part = work.tile([P, CHUNK], F32, name=f"part{t}")
+                nc.vector.tensor_tensor(
+                    part[:],
+                    y[b][:].indirect(lst[:, v0 // LANES : (v0 + CHUNK) // LANES]),
+                    fac[:, v0 : v0 + CHUNK],
+                    ALU.mult,
+                )
+                parts.append(part)
+            res = work.tile([P, CHUNK], F32, name="res")
+            if (b, v0) == chunks[-1]:
+                pair = keep.tile([P, CHUNK], F32, name="pair")
+                nc.vector.tensor_tensor(pair[:], parts[0][:], parts[1][:], ALU.add)
+                nc.vector.tensor_tensor(res[:], pair[:], parts[2][:], ALU.add)
+            else:
+                there = turn.tile([P, CHUNK], F32, name="there")
+                for c in range(0, CHUNK, P):
+                    for t in range(3):
+                        nc.tensor.matmul(
+                            there[:, c : c + P], parts[t][:, c : c + P], ident[:],
+                            start=(t == 0), stop=(t == 2), is_transpose=True,
+                        )
+                summed = work.tile([P, CHUNK], F32, name="summed")
+                nc.scalar.copy(summed[:], there[:])
+                back = turn.tile([P, CHUNK], F32, name="back")
+                for c in range(0, CHUNK, P):
+                    nc.tensor.transpose(back[:, c : c + P], summed[:, c : c + P], ident[:])
+                nc.scalar.copy(res[:], back[:])
+            nc.sync.dma_start(out[b * P : (b + 1) * P, v0 : v0 + CHUNK], res[:])

@@ -20,26 +20,24 @@ P = 128
 PACK = 4
 LANES = 16
 QUAD = 32
-BANK = 512
-CHUNK = 256
+PIECE = 256
 
 
 def tile_picked_grand_relu_p_kernel(tc, x_words, x_scales, w1, gate, offs, cen, pos1, pos2, out):
     nc = tc.nc
     with ExitStack() as ctx:
         keep = ctx.enter_context(tc.tile_pool(name="keep", bufs=1))
-        work = ctx.enter_context(tc.tile_pool(name="work", bufs=2))
         psum = ctx.enter_context(tc.psum_pool(name="psum", bufs=1))
-        turn = ctx.enter_context(tc.psum_pool(name="turn", bufs=2))
 
         offs_t = keep.tile([P, S // LANES], U16, name="offs_t")
         cen_t = keep.tile([P, V // LANES], U16, name="cen_t")
         pos1_t = keep.tile([P, V // LANES], U16, name="pos1_t")
         pos2_t = keep.tile([P, V // LANES], U16, name="pos2_t")
         scale_tab = keep.tile([P, T], U8, name="scale_tab", align_bytes=64)
-        word_tab = keep.tile([P, T], I32, name="word_tab", align_bytes=64)
-        w_raw = keep.tile([P, PACK, N], F32, name="w_raw")
+        word_tab = keep.tile([P, T], I32, name="word_tab", tag="word_tab", align_bytes=64)
         gate_t = keep.tile([P, 2, V], F32, name="gate_t")
+        w_rows = w1.rearrange("(p j) m -> p j m", j=PACK)
+        w_raw = [keep.tile([P, PACK, P], F32, name=f"w_raw{b}", tag=f"w_raw{b}", align_bytes=64) for b in range(N // P)]
 
         nc.sync.dma_start(offs_t[:], offs)
         for q in range(P // QUAD):
@@ -49,7 +47,8 @@ def tile_picked_grand_relu_p_kernel(tc, x_words, x_scales, w1, gate, offs, cen, 
                 rows.unsqueeze(0).broadcast_to([QUAD // PACK, PACK, T // 4]),
             )
         nc.sync.dma_start(word_tab[:], x_words[0].rearrange("p n t -> p (n t)").bitcast(I32))
-        nc.sync.dma_start(w_raw[:], w1.rearrange("(p j) m -> p j m", j=PACK))
+        nc.sync.dma_start(w_raw[0][:], w_rows[:, :, :P])
+        nc.sync.dma_start(w_raw[1][:], w_rows[:, :, P:])
         nc.sync.dma_start(gate_t[:], gate.rearrange("d p v -> p d v"))
         nc.sync.dma_start(pos1_t[:], pos1)
         nc.sync.dma_start(pos2_t[:], pos2)
@@ -61,77 +60,112 @@ def tile_picked_grand_relu_p_kernel(tc, x_words, x_scales, w1, gate, offs, cen, 
         x_scale = keep.tile([P, S], U8, name="x_scale", align_bytes=64)
         nc.vector.tensor_copy(x_scale[:], scale_tab[:].indirect(offs_t[:]))
 
-        w_codes, w_scale = [], []
-        for b in range(N // P):
-            grouped = keep.tile([P, P, PACK], BF16, name=f"grouped{b}", align_bytes=64)
-            nc.scalar.copy(grouped[:], w_raw[:, :, b * P : (b + 1) * P].rearrange("p j m -> p m j"))
+        grouped, w_codes, w_scale = [], [], []
+
+        def cast(b):
+            grouped.append(keep.tile([P, P, PACK], BF16, name=f"grouped{b}", align_bytes=64))
+            nc.scalar.copy(grouped[b][:], w_raw[b][:].rearrange("p j m -> p m j"))
+
+        def quantise(b):
             w_codes.append(keep.tile([P, P], U32, name=f"w_codes{b}", align_bytes=64))
             w_scale.append(keep.tile([P, P], U8, name=f"w_scale{b}", align_bytes=64))
             nc.vector.quantize_mx(
                 out=w_codes[b][:].bitcast(FP8X4),
                 scales=w_scale[b][:],
-                in_=grouped[:].rearrange("p m j -> p (m j)"),
+                in_=grouped[b][:].rearrange("p m j -> p (m j)"),
             )
 
-        x_codes = keep.tile([P, S], U32, name="x_codes", align_bytes=64)
-        pieces = [(0, 512), (512, 768), (768, 1024)]
-        for a, z in pieces:
+        cast(0)
+        quantise(0)
+        cast(1)
+        halves = [
+            keep.tile([P, S // 2], U32, name=f"x_codes{h}", tag=tag, align_bytes=64)
+            for h, tag in enumerate(["x_codes0", "w_raw0"])
+        ]
+        x_codes = [halves[i // 2][:, i % 2 * PIECE : (i % 2 + 1) * PIECE] for i in range(S // PIECE)]
+        for i in range(S // PIECE):
             nc.vector.tensor_copy(
-                x_codes[:, a:z], word_tab[:].bitcast(U32).indirect(offs_t[:, a // LANES : z // LANES])
+                x_codes[i],
+                word_tab[:].bitcast(U32).indirect(offs_t[:, i * PIECE // LANES : (i + 1) * PIECE // LANES]),
             )
+        quantise(1)
 
-        keepc = keep.tile([P, V], F32, name="keepc")
-        one_less = keep.tile([P, V], F32, name="one_less")
-        nc.scalar.activation(one_less[:], gate_t[:, 0, :], ACT.Copy, bias=1.0, scale=-1.0)
+        minus_own = keep.tile([P, V], F32, name="minus_own", tag="word_tab", align_bytes=64)
+        own = keep.tile([P, V], F32, name="own")
+        nc.vector.scalar_tensor_tensor(minus_own[:], gate_t[:, 0, :], 1.0, gate_t[:, 1, :], ALU.subtract, ALU.add)
+        factor = [gate_t[:, 0, :], gate_t[:, 1, :], own[:]]
 
-        y = []
-        for b in range(N // P):
-            y.append(keep.tile([P, S], F32, name=f"y{b}"))
-            for i, (a, z) in enumerate(pieces if b == 0 else [(0, 512), (512, 1024)]):
-                acc = psum.tile([P, z - a], F32, name=f"acc{b}_{i}", tag=f"acc{(3 * b + i) % 4}")
+        y = [keep.tile([P, S], F32, name=f"y{b}") for b in range(N // P)]
+
+        def product(b, spans, bank, on_vector=False):
+            a0, z0 = spans[0][0], spans[-1][1]
+            acc = psum.tile([P, z0 - a0], F32, name=f"acc{b}_{a0}", tag=f"bank{bank}")
+            for a, z in spans:
+                i, off = divmod(a, PIECE)
                 nc.tensor.matmul_mx(
-                    out=acc[:],
+                    out=acc[:, a - a0 : z - a0],
                     lhsT=w_codes[b][:].bitcast(FP8X4),
                     lhsT_scale=w_scale[b][:],
-                    rhs=x_codes[:, a:z].bitcast(FP8X4),
+                    rhs=x_codes[i][:, off : off + z - a].bitcast(FP8X4),
                     rhs_scale=x_scale[:, a:z],
                     start=True,
                     stop=True,
                 )
-                nc.scalar.activation(y[b][:, a:z], acc[:], ACT.Relu)
-
-        nc.vector.tensor_tensor(keepc[:], one_less[:], gate_t[:, 1, :], ALU.subtract)
-
-        terms = [(pos1_t, gate_t[:, 0, :]), (pos2_t, gate_t[:, 1, :]), (cen_t, keepc[:])]
-        chunks = [(b, v0) for b in range(N // P) for v0 in range(0, V, CHUNK)]
-        for b, v0 in chunks:
-            parts = []
-            for t, (lst, fac) in enumerate(terms):
-                part = work.tile([P, CHUNK], F32, name=f"part{t}")
-                nc.vector.tensor_tensor(
-                    part[:],
-                    y[b][:].indirect(lst[:, v0 // LANES : (v0 + CHUNK) // LANES]),
-                    fac[:, v0 : v0 + CHUNK],
-                    ALU.mult,
-                )
-                parts.append(part)
-            res = work.tile([P, CHUNK], F32, name="res")
-            if (b, v0) == chunks[-1]:
-                pair = keep.tile([P, CHUNK], F32, name="pair")
-                nc.vector.tensor_tensor(pair[:], parts[0][:], parts[1][:], ALU.add)
-                nc.vector.tensor_tensor(res[:], pair[:], parts[2][:], ALU.add)
+            if on_vector:
+                nc.vector.tensor_scalar_max(y[b][:, a0:z0], acc[:], 0.0)
             else:
-                there = turn.tile([P, CHUNK], F32, name="there")
-                for c in range(0, CHUNK, P):
-                    for t in range(3):
-                        nc.tensor.matmul(
-                            there[:, c : c + P], parts[t][:, c : c + P], ident[:],
-                            start=(t == 0), stop=(t == 2), is_transpose=True,
-                        )
-                summed = work.tile([P, CHUNK], F32, name="summed")
-                nc.scalar.copy(summed[:], there[:])
-                back = turn.tile([P, CHUNK], F32, name="back")
-                for c in range(0, CHUNK, P):
-                    nc.tensor.transpose(back[:, c : c + P], summed[:, c : c + P], ident[:])
-                nc.scalar.copy(res[:], back[:])
-            nc.sync.dma_start(out[b * P : (b + 1) * P, v0 : v0 + CHUNK], res[:])
+                nc.scalar.activation(y[b][:, a0:z0], acc[:], ACT.Relu)
+
+        product(0, [(0, 256)], 0)
+        product(0, [(256, 512)], 1)
+        product(0, [(512, 768)], 2)
+        product(0, [(768, 896)], 5)
+        product(0, [(896, 1024)], 6, True)
+        nc.scalar.mul(own[:], minus_own[:], -1.0)
+        product(1, [(0, 256), (256, 512)], 3)
+        product(1, [(512, 768), (768, 1024)], 4)
+
+        lists = [pos1_t, pos2_t, cen_t]
+        banks = [7, 5, 6, 0, 1, 2, 3, 4, 5, 6, 7, 0, 1, 2, 3]
+
+        def term(b, t, v0, v1):
+            part = keep.tile([P, v1 - v0], F32, name=f"part{b}_{t}_{v0}")
+            nc.vector.tensor_tensor(
+                part[:], y[b][:].indirect(lists[t][:, v0 // LANES : v1 // LANES]), factor[t][:, v0:v1], ALU.mult
+            )
+            return part
+
+        def add_on_tensor(parts, name):
+            width = parts[0].shape[1]
+            theres = [
+                psum.tile([P, P], F32, name=f"there{name}_{c}", tag=f"bank{banks.pop(0)}") for c in range(0, width, P)
+            ]
+            for t, part in enumerate(parts):
+                for i, there in enumerate(theres):
+                    nc.tensor.matmul(
+                        there[:], part[:, i * P : (i + 1) * P], ident[:],
+                        start=(t == 0), stop=(t == len(parts) - 1), is_transpose=True,
+                    )
+            summed = keep.tile([P, width], F32, name=f"summed{name}")
+            for i, there in enumerate(theres):
+                nc.scalar.copy(summed[:, i * P : (i + 1) * P], there[:])
+            back = psum.tile([P, width], F32, name=f"back{name}", tag=f"bank{banks.pop(0)}")
+            for c in range(0, width, P):
+                nc.tensor.transpose(back[:, c : c + P], summed[:, c : c + P], ident[:])
+            return back
+
+        def whole_chunk(b, v0, v1):
+            back = add_on_tensor([term(b, t, v0, v1)[:] for t in range(3)], f"{b}_{v0}")
+            res = keep.tile([P, v1 - v0], F32, name=f"res{b}_{v0}")
+            nc.scalar.copy(res[:], back[:])
+            nc.sync.dma_start(out[b * P : (b + 1) * P, v0:v1], res[:])
+
+        whole_chunk(0, 0, 256)
+        whole_chunk(0, 256, 512)
+        whole_chunk(1, 0, 256)
+        parts = [term(1, t, 256, 512) for t in range(3)]
+        pair = keep.tile([P, 256], F32, name="pair")
+        res = keep.tile([P, 256], F32, name="res")
+        nc.vector.tensor_tensor(pair[:], parts[0][:], parts[1][:], ALU.add)
+        nc.vector.tensor_tensor(res[:], pair[:], parts[2][:], ALU.add)
+        nc.sync.dma_start(out[P:, 256:], res[:])

@@ -39,19 +39,20 @@ def tile_picked_grand_relu_p_kernel(tc, x_words, x_scales, w1, gate, offs, cen, 
         w_rows = w1.rearrange("(p j) m -> p j m", j=PACK)
         w_raw = [keep.tile([P, PACK, P], F32, name=f"w_raw{b}", tag=f"w_raw{b}", align_bytes=64) for b in range(N // P)]
 
+        nc.vector.memset(scale_tab[:, : T // 2].bitcast(I32), 0)
+        nc.gpsimd.memset(scale_tab[:, T // 2 :].bitcast(I32), 0)
         nc.sync.dma_start(offs_t[:], offs)
+        nc.sync.dma_start(pos1_t[:], pos1)
+        nc.sync.dma_start(pos2_t[:], pos2)
         for q in range(P // QUAD):
-            rows = x_scales[0, PACK * q : PACK * (q + 1), :].bitcast(I32)
             nc.sync.dma_start(
-                scale_tab[QUAD * q : QUAD * (q + 1), :].bitcast(I32),
-                rows.unsqueeze(0).broadcast_to([QUAD // PACK, PACK, T // 4]),
+                scale_tab[QUAD * q : QUAD * q + PACK, :].bitcast(I32),
+                x_scales[0, PACK * q : PACK * (q + 1), :].bitcast(I32),
             )
         nc.sync.dma_start(word_tab[:], x_words[0].rearrange("p n t -> p (n t)").bitcast(I32))
         nc.sync.dma_start(w_raw[0][:], w_rows[:, :, :P])
         nc.sync.dma_start(w_raw[1][:], w_rows[:, :, P:])
         nc.sync.dma_start(gate_t[:], gate.rearrange("d p v -> p d v"))
-        nc.sync.dma_start(pos1_t[:], pos1)
-        nc.sync.dma_start(pos2_t[:], pos2)
         nc.sync.dma_start(cen_t[:], cen)
 
         ident = keep.tile([P, P], F32, name="ident")

@@ -127,7 +127,7 @@ def tile_picked_grand_relu_p_kernel(tc, x_words, x_scales, w1, gate, offs, cen, 
         product(1, [(512, 768), (768, 1024)], 4)
 
         lists = [pos1_t, pos2_t, cen_t]
-        banks = [7, 5, 6, 0, 1, 2, 3, 4, 5, 6, 7, 0, 1, 2, 3]
+        banks = [7, 0, 1, 2, 5, 7, 0, 6]
 
         def term(b, t, v0, v1):
             part = keep.tile([P, v1 - v0], F32, name=f"part{b}_{t}_{v0}")
@@ -159,10 +159,9 @@ def tile_picked_grand_relu_p_kernel(tc, x_words, x_scales, w1, gate, offs, cen, 
             back = add_on_tensor([term(b, t, v0, v1)[:] for t in range(3)], f"{b}_{v0}")
             res = keep.tile([P, v1 - v0], F32, name=f"res{b}_{v0}")
             nc.scalar.copy(res[:], back[:])
-            nc.sync.dma_start(out[b * P : (b + 1) * P, v0:v1], res[:])
+            nc.scalar.dma_start(out[b * P : (b + 1) * P, v0:v1], res[:])
 
-        whole_chunk(0, 0, 256)
-        whole_chunk(0, 256, 512)
+        whole_chunk(0, 0, 512)
         whole_chunk(1, 0, 256)
         parts = [term(1, t, 256, 512) for t in range(3)]
         pair = keep.tile([P, 256], F32, name="pair")

@@ -65,7 +65,10 @@ def tile_picked_grand_relu_p_kernel(tc, x_words, x_scales, w1, gate, offs, cen, 
 
         def cast(b):
             grouped.append(keep.tile([P, P, PACK], BF16, name=f"grouped{b}", align_bytes=64))
-            nc.scalar.copy(grouped[b][:], w_raw[b][:].rearrange("p j m -> p m j"))
+            nc.scalar.copy(
+                grouped[b][:].rearrange("p (c i) j -> p c j i", i=PACK),
+                w_raw[b][:].rearrange("p j (c i) -> p c j i", i=PACK),
+            )
 
         def quantise(b):
             w_codes.append(keep.tile([P, P], U32, name=f"w_codes{b}", align_bytes=64))
@@ -84,7 +87,8 @@ def tile_picked_grand_relu_p_kernel(tc, x_words, x_scales, w1, gate, offs, cen, 
             for h, tag in enumerate(["x_codes0", "w_raw0"])
         ]
         x_codes = [halves[i // 2][:, i % 2 * PIECE : (i % 2 + 1) * PIECE] for i in range(S // PIECE)]
-        for i in range(S // PIECE):
+        nc.vector.tensor_copy(halves[0][:], word_tab[:].bitcast(U32).indirect(offs_t[:, : S // 2 // LANES]))
+        for i in range(2, S // PIECE):
             nc.vector.tensor_copy(
                 x_codes[i],
                 word_tab[:].bitcast(U32).indirect(offs_t[:, i * PIECE // LANES : (i + 1) * PIECE // LANES]),
@@ -164,8 +168,10 @@ def tile_picked_grand_relu_p_kernel(tc, x_words, x_scales, w1, gate, offs, cen, 
         whole_chunk(0, 0, 512)
         whole_chunk(1, 0, 256)
         parts = [term(1, t, 256, 512) for t in range(3)]
-        pair = keep.tile([P, 256], F32, name="pair")
-        res = keep.tile([P, 256], F32, name="res")
-        nc.vector.tensor_tensor(pair[:], parts[0][:], parts[1][:], ALU.add)
-        nc.vector.tensor_tensor(res[:], pair[:], parts[2][:], ALU.add)
-        nc.sync.dma_start(out[P:, 256:], res[:])
+        pairs = [keep.tile([P, P], F32, name=f"pair{h}") for h in range(2)]
+        for h in range(2):
+            nc.vector.tensor_tensor(pairs[h][:], parts[0][:, h * P : (h + 1) * P], parts[1][:, h * P : (h + 1) * P], ALU.add)
+        for h in range(2):
+            res = keep.tile([P, P], F32, name=f"last{h}")
+            nc.vector.tensor_tensor(res[:], pairs[h][:], parts[2][:, h * P : (h + 1) * P], ALU.add)
+            nc.sync.dma_start(out[P:, 256 + h * P : 256 + (h + 1) * P], res[:])

@@ -44,11 +44,8 @@ def tile_picked_grand_relu_p_kernel(tc, x_words, x_scales, w1, gate, offs, cen, 
         nc.sync.dma_start(offs_t[:], offs)
         nc.sync.dma_start(pos1_t[:], pos1)
         nc.sync.dma_start(pos2_t[:], pos2)
-        for q in range(P // QUAD):
-            nc.sync.dma_start(
-                scale_tab[QUAD * q : QUAD * q + PACK, :].bitcast(I32),
-                x_scales[0, PACK * q : PACK * (q + 1), :].bitcast(I32),
-            )
+        for r in range(PACK):
+            nc.sync.dma_start(scale_tab[r:P:QUAD, :].bitcast(I32), x_scales[0, r::PACK, :].bitcast(I32))
         nc.sync.dma_start(word_tab[:], x_words[0].rearrange("p n t -> p (n t)").bitcast(I32))
         nc.sync.dma_start(w_raw[0][:], w_rows[:, :, :P])
         nc.sync.dma_start(w_raw[1][:], w_rows[:, :, P:])

@@ -42,15 +42,16 @@ def tile_picked_grand_relu_p_kernel(tc, x_words, x_scales, w1, gate, offs, cen, 
         nc.vector.memset(scale_tab[:, : T // 2].bitcast(I32), 0)
         nc.gpsimd.memset(scale_tab[:, T // 2 :].bitcast(I32), 0)
         nc.sync.dma_start(offs_t[:], offs)
-        nc.sync.dma_start(pos1_t[:], pos1)
-        nc.sync.dma_start(pos2_t[:], pos2)
+        nc.sync.dma_start(w_raw[0][:, :2, :], w_rows[:, :2, :P])
+        nc.sync.dma_start(cen_t[:], cen)
         for r in range(PACK):
             nc.sync.dma_start(scale_tab[r:P:QUAD, :].bitcast(I32), x_scales[0, r::PACK, :].bitcast(I32))
         nc.sync.dma_start(word_tab[:], x_words[0].rearrange("p n t -> p (n t)").bitcast(I32))
-        nc.sync.dma_start(w_raw[0][:], w_rows[:, :, :P])
+        nc.sync.dma_start(w_raw[0][:, 2:, :], w_rows[:, 2:, :P])
         nc.sync.dma_start(w_raw[1][:], w_rows[:, :, P:])
         nc.sync.dma_start(gate_t[:], gate.rearrange("d p v -> p d v"))
-        nc.sync.dma_start(cen_t[:], cen)
+        nc.sync.dma_start(pos1_t[:], pos1)
+        nc.sync.dma_start(pos2_t[:], pos2)
 
         ident = keep.tile([P, P], F32, name="ident")
         make_identity(nc, ident[:])
@@ -128,7 +129,6 @@ def tile_picked_grand_relu_p_kernel(tc, x_words, x_scales, w1, gate, offs, cen, 
         product(1, [(512, 768), (768, 1024)], 4)
 
         lists = [pos1_t, pos2_t, cen_t]
-        banks = [7, 0, 1, 2, 5, 7, 0, 6]
 
         def term(b, t, v0, v1):
             part = keep.tile([P, v1 - v0], F32, name=f"part{b}_{t}_{v0}")
@@ -137,33 +137,38 @@ def tile_picked_grand_relu_p_kernel(tc, x_words, x_scales, w1, gate, offs, cen, 
             )
             return part
 
-        def add_on_tensor(parts, name):
-            width = parts[0].shape[1]
-            theres = [
-                psum.tile([P, P], F32, name=f"there{name}_{c}", tag=f"bank{banks.pop(0)}") for c in range(0, width, P)
-            ]
-            for t, part in enumerate(parts):
-                for i, there in enumerate(theres):
-                    nc.tensor.matmul(
-                        there[:], part[:, i * P : (i + 1) * P], ident[:],
-                        start=(t == 0), stop=(t == len(parts) - 1), is_transpose=True,
-                    )
+        def banks(numbers, name):
+            return [psum.tile([P, P], F32, name=f"there{name}_{n}", tag=f"bank{n}") for n in numbers]
+
+        def turn_in(theres, part, first, last):
+            for i, there in enumerate(theres):
+                nc.tensor.matmul(
+                    there[:], part[:, i * P : (i + 1) * P], ident[:], start=first, stop=last, is_transpose=True
+                )
+
+        def turn_back(theres, number, res, name):
+            width = len(theres) * P
             summed = keep.tile([P, width], F32, name=f"summed{name}")
             for i, there in enumerate(theres):
                 nc.scalar.copy(summed[:, i * P : (i + 1) * P], there[:])
-            back = psum.tile([P, width], F32, name=f"back{name}", tag=f"bank{banks.pop(0)}")
+            back = psum.tile([P, width], F32, name=f"back{name}", tag=f"bank{number}")
             for c in range(0, width, P):
                 nc.tensor.transpose(back[:, c : c + P], summed[:, c : c + P], ident[:])
-            return back
+            nc.scalar.copy(res, back[:])
 
-        def whole_chunk(b, v0, v1):
-            back = add_on_tensor([term(b, t, v0, v1)[:] for t in range(3)], f"{b}_{v0}")
-            res = keep.tile([P, v1 - v0], F32, name=f"res{b}_{v0}")
-            nc.scalar.copy(res[:], back[:])
-            nc.scalar.dma_start(out[b * P : (b + 1) * P, v0:v1], res[:])
-
-        whole_chunk(0, 0, 512)
-        whole_chunk(1, 0, 256)
+        there0 = banks((7, 0, 1, 2), "0")
+        res0 = keep.tile([P, V], F32, name="res0")
+        for h in range(2):
+            for t in range(3):
+                turn_in(there0[2 * h : 2 * h + 2], term(0, t, h * 256, (h + 1) * 256), t == 0, t == 2)
+            turn_back(there0[2 * h : 2 * h + 2], 5 + h, res0[:, h * 256 : (h + 1) * 256], f"0_{h}")
+        nc.scalar.dma_start(out[:P, :], res0[:])
+        there1 = banks((3, 4), "1")
+        for t in range(3):
+            turn_in(there1, term(1, t, 0, 256), t == 0, t == 2)
+        res1 = keep.tile([P, 256], F32, name="res1")
+        turn_back(there1, 7, res1[:], "1")
+        nc.scalar.dma_start(out[P:, :256], res1[:])
         parts = [term(1, t, 256, 512) for t in range(3)]
         pairs = [keep.tile([P, P], F32, name=f"pair{h}") for h in range(2)]
         for h in range(2):

@@ -20,7 +20,8 @@ P = 128
 PACK = 4
 LANES = 16
 QUAD = 32
-PIECE = 256
+CUT = 768
+FIRST = P - K // 32
 
 
 def tile_picked_grand_relu_p_kernel(tc, x_words, x_scales, w1, gate, offs, cen, pos1, pos2, out):
@@ -39,30 +40,30 @@ def tile_picked_grand_relu_p_kernel(tc, x_words, x_scales, w1, gate, offs, cen, 
         w_rows = w1.rearrange("(p j) m -> p j m", j=PACK)
         w_raw = [keep.tile([P, PACK, P], F32, name=f"w_raw{b}", tag=f"w_raw{b}", align_bytes=64) for b in range(N // P)]
 
-        nc.vector.memset(scale_tab[:, : T // 2].bitcast(I32), 0)
-        nc.gpsimd.memset(scale_tab[:, T // 2 :].bitcast(I32), 0)
+        nc.vector.memset(scale_tab[:FIRST, :].bitcast(I32), 0)
+        nc.sync.dma_start(scale_tab[FIRST:, :].bitcast(I32), x_scales[0].bitcast(I32))
         nc.sync.dma_start(offs_t[:], offs)
-        nc.sync.dma_start(w_raw[0][:, :2, :], w_rows[:, :2, :P])
-        nc.sync.dma_start(cen_t[:], cen)
-        for r in range(PACK):
-            nc.sync.dma_start(scale_tab[r:P:QUAD, :].bitcast(I32), x_scales[0, r::PACK, :].bitcast(I32))
         nc.sync.dma_start(word_tab[:], x_words[0].rearrange("p n t -> p (n t)").bitcast(I32))
-        nc.sync.dma_start(w_raw[0][:, 2:, :], w_rows[:, 2:, :P])
-        nc.sync.dma_start(w_raw[1][:], w_rows[:, :, P:])
-        nc.sync.dma_start(gate_t[:], gate.rearrange("d p v -> p d v"))
+        nc.sync.dma_start(cen_t[:], cen)
         nc.sync.dma_start(pos1_t[:], pos1)
+        nc.sync.dma_start(w_raw[0][:], w_rows[:, :, :P])
+        nc.sync.dma_start(gate_t[:], gate.rearrange("d p v -> p d v"))
+        nc.sync.dma_start(w_raw[1][:], w_rows[:, :, P:])
         nc.sync.dma_start(pos2_t[:], pos2)
 
         ident = keep.tile([P, P], F32, name="ident")
         make_identity(nc, ident[:])
 
+        picked = keep.tile([P, S], U8, name="picked", align_bytes=64)
+        nc.vector.tensor_copy(picked[:], scale_tab[:].indirect(offs_t[:]))
         x_scale = keep.tile([P, S], U8, name="x_scale", align_bytes=64)
-        nc.vector.tensor_copy(x_scale[:], scale_tab[:].indirect(offs_t[:]))
+        for r in range(PACK):
+            nc.sync.dma_start(x_scale[r:P:QUAD, :].bitcast(I32), picked[FIRST + r : P : PACK, :].bitcast(I32))
 
         grouped, w_codes, w_scale = [], [], []
 
         def cast(b):
-            grouped.append(keep.tile([P, P, PACK], BF16, name=f"grouped{b}", align_bytes=64))
+            grouped.append(keep.tile([P, P, PACK], BF16, name=f"grouped{b}", tag=f"grouped{b}", align_bytes=64))
             nc.scalar.copy(
                 grouped[b][:].rearrange("p (c i) j -> p c j i", i=PACK),
                 w_raw[b][:].rearrange("p j (c i) -> p c j i", i=PACK),
@@ -80,22 +81,16 @@ def tile_picked_grand_relu_p_kernel(tc, x_words, x_scales, w1, gate, offs, cen, 
         cast(0)
         quantise(0)
         cast(1)
-        halves = [
-            keep.tile([P, S // 2], U32, name=f"x_codes{h}", tag=tag, align_bytes=64)
-            for h, tag in enumerate(["x_codes0", "w_raw0"])
-        ]
-        x_codes = [halves[i // 2][:, i % 2 * PIECE : (i % 2 + 1) * PIECE] for i in range(S // PIECE)]
-        nc.vector.tensor_copy(halves[0][:], word_tab[:].bitcast(U32).indirect(offs_t[:, : S // 2 // LANES]))
-        for i in range(2, S // PIECE):
-            nc.vector.tensor_copy(
-                x_codes[i],
-                word_tab[:].bitcast(U32).indirect(offs_t[:, i * PIECE // LANES : (i + 1) * PIECE // LANES]),
-            )
+        x_codes = []
+        for a, z, tag in ((0, CUT, "x_codes0"), (CUT, S, "grouped0")):
+            x_codes.append(keep.tile([P, z - a], U32, name=f"x_codes{a}", tag=tag, align_bytes=64))
+            nc.vector.tensor_copy(x_codes[-1][:], word_tab[:].bitcast(U32).indirect(offs_t[:, a // LANES : z // LANES]))
         quantise(1)
 
-        minus_own = keep.tile([P, V], F32, name="minus_own", tag="word_tab", align_bytes=64)
-        own = keep.tile([P, V], F32, name="own")
-        nc.vector.scalar_tensor_tensor(minus_own[:], gate_t[:, 0, :], 1.0, gate_t[:, 1, :], ALU.subtract, ALU.add)
+        rest = keep.tile([P, V], F32, name="rest")
+        nc.scalar.activation(rest[:], gate_t[:, 0, :], ACT.Identity, bias=1.0, scale=-1.0)
+        own = keep.tile([P, V], F32, name="own", tag="word_tab", align_bytes=64)
+        nc.vector.tensor_tensor(own[:], rest[:], gate_t[:, 1, :], ALU.subtract)
         factor = [gate_t[:, 0, :], gate_t[:, 1, :], own[:]]
 
         y = [keep.tile([P, S], F32, name=f"y{b}") for b in range(N // P)]
@@ -104,7 +99,7 @@ def tile_picked_grand_relu_p_kernel(tc, x_words, x_scales, w1, gate, offs, cen, 
             a0, z0 = spans[0][0], spans[-1][1]
             acc = psum.tile([P, z0 - a0], F32, name=f"acc{b}_{a0}", tag=f"bank{bank}")
             for a, z in spans:
-                i, off = divmod(a, PIECE)
+                i, off = divmod(a, CUT)
                 nc.tensor.matmul_mx(
                     out=acc[:, a - a0 : z - a0],
                     lhsT=w_codes[b][:].bitcast(FP8X4),
@@ -121,11 +116,10 @@ def tile_picked_grand_relu_p_kernel(tc, x_words, x_scales, w1, gate, offs, cen, 
 
         product(0, [(0, 256)], 0)
         product(0, [(256, 512)], 1)
-        product(0, [(512, 768)], 2)
+        product(0, [(512, 768)], 2, True)
         product(0, [(768, 896)], 5)
         product(0, [(896, 1024)], 6, True)
-        nc.scalar.mul(own[:], minus_own[:], -1.0)
-        product(1, [(0, 256), (256, 512)], 3)
+        product(1, [(0, 512)], 3)
         product(1, [(512, 768), (768, 1024)], 4)
 
         lists = [pos1_t, pos2_t, cen_t]

@@ -21,6 +21,7 @@ PACK = 4
 LANES = 16
 QUAD = 32
 CUT = 768
+HALF = V // 2
 FIRST = P - K // 32
 
 
@@ -34,11 +35,9 @@ def tile_picked_grand_relu_p_kernel(tc, x_words, x_scales, w1, gate, offs, cen, 
         cen_t = keep.tile([P, V // LANES], U16, name="cen_t")
         pos1_t = keep.tile([P, V // LANES], U16, name="pos1_t")
         pos2_t = keep.tile([P, V // LANES], U16, name="pos2_t")
-        scale_tab = keep.tile([P, T], U8, name="scale_tab", align_bytes=64)
+        scale_tab = keep.tile([P, T], U8, name="scale_tab", tag="scale_tab", align_bytes=64)
         word_tab = keep.tile([P, T], I32, name="word_tab", tag="word_tab", align_bytes=64)
-        gate_t = keep.tile([P, 2, V], F32, name="gate_t")
-        w_rows = w1.rearrange("(p j) m -> p j m", j=PACK)
-        w_raw = [keep.tile([P, PACK, P], F32, name=f"w_raw{b}", tag=f"w_raw{b}", align_bytes=64) for b in range(N // P)]
+        w_raw = keep.tile([P, PACK, N], F32, name="w_raw")
 
         nc.vector.memset(scale_tab[:FIRST, :].bitcast(I32), 0)
         nc.sync.dma_start(scale_tab[FIRST:, :].bitcast(I32), x_scales[0].bitcast(I32))
@@ -46,10 +45,11 @@ def tile_picked_grand_relu_p_kernel(tc, x_words, x_scales, w1, gate, offs, cen, 
         nc.sync.dma_start(word_tab[:], x_words[0].rearrange("p n t -> p (n t)").bitcast(I32))
         nc.sync.dma_start(cen_t[:], cen)
         nc.sync.dma_start(pos1_t[:], pos1)
-        nc.sync.dma_start(w_raw[0][:], w_rows[:, :, :P])
-        nc.sync.dma_start(gate_t[:], gate.rearrange("d p v -> p d v"))
-        nc.sync.dma_start(w_raw[1][:], w_rows[:, :, P:])
         nc.sync.dma_start(pos2_t[:], pos2)
+        nc.sync.dma_start(w_raw[:], w1.rearrange("(p j) m -> p j m", j=PACK))
+        gate_rows = gate.rearrange("d p v -> p d v")
+        gates = [keep.tile([P, 2, HALF], F32, name="gates0")]
+        nc.sync.dma_start(gates[0][:], gate_rows[:, :, :HALF])
 
         ident = keep.tile([P, P], F32, name="ident")
         make_identity(nc, ident[:])
@@ -60,17 +60,20 @@ def tile_picked_grand_relu_p_kernel(tc, x_words, x_scales, w1, gate, offs, cen, 
         for r in range(PACK):
             nc.sync.dma_start(x_scale[r:P:QUAD, :].bitcast(I32), picked[FIRST + r : P : PACK, :].bitcast(I32))
 
+        gates.append(keep.tile([P, 2, HALF], F32, name="gates1", tag="scale_tab", align_bytes=64))
+        nc.sync.dma_start(gates[1][:], gate_rows[:, :, HALF:])
+
         grouped, w_codes, w_scale = [], [], []
 
         def cast(b):
             grouped.append(keep.tile([P, P, PACK], BF16, name=f"grouped{b}", tag=f"grouped{b}", align_bytes=64))
             nc.scalar.copy(
                 grouped[b][:].rearrange("p (c i) j -> p c j i", i=PACK),
-                w_raw[b][:].rearrange("p j (c i) -> p c j i", i=PACK),
+                w_raw[:, :, b * P : (b + 1) * P].rearrange("p j (c i) -> p c j i", i=PACK),
             )
 
         def quantise(b):
-            w_codes.append(keep.tile([P, P], U32, name=f"w_codes{b}", align_bytes=64))
+            w_codes.append(keep.tile([P, P], U32, name=f"w_codes{b}", tag=f"w_codes{b}", align_bytes=64))
             w_scale.append(keep.tile([P, P], U8, name=f"w_scale{b}", align_bytes=64))
             nc.vector.quantize_mx(
                 out=w_codes[b][:].bitcast(FP8X4),
@@ -87,11 +90,8 @@ def tile_picked_grand_relu_p_kernel(tc, x_words, x_scales, w1, gate, offs, cen, 
             nc.vector.tensor_copy(x_codes[-1][:], word_tab[:].bitcast(U32).indirect(offs_t[:, a // LANES : z // LANES]))
         quantise(1)
 
-        rest = keep.tile([P, V], F32, name="rest")
-        nc.scalar.activation(rest[:], gate_t[:, 0, :], ACT.Identity, bias=1.0, scale=-1.0)
-        own = keep.tile([P, V], F32, name="own", tag="word_tab", align_bytes=64)
-        nc.vector.tensor_tensor(own[:], rest[:], gate_t[:, 1, :], ALU.subtract)
-        factor = [gate_t[:, 0, :], gate_t[:, 1, :], own[:]]
+        minus_own = keep.tile([P, V], F32, name="minus_own", tag="word_tab", align_bytes=64)
+        own = keep.tile([P, V], F32, name="own", tag="w_codes0", align_bytes=64)
 
         y = [keep.tile([P, S], F32, name=f"y{b}") for b in range(N // P)]
 
@@ -119,6 +119,11 @@ def tile_picked_grand_relu_p_kernel(tc, x_words, x_scales, w1, gate, offs, cen, 
         product(0, [(512, 768)], 2, True)
         product(0, [(768, 896)], 5)
         product(0, [(896, 1024)], 6, True)
+        for h in range(2):
+            nc.vector.scalar_tensor_tensor(
+                minus_own[:, h * HALF : (h + 1) * HALF], gates[h][:, 0, :], 1.0, gates[h][:, 1, :], ALU.subtract, ALU.add
+            )
+        nc.scalar.mul(own[:], minus_own[:], -1.0)
         product(1, [(0, 512)], 3)
         product(1, [(512, 768), (768, 1024)], 4)
 
@@ -126,9 +131,8 @@ def tile_picked_grand_relu_p_kernel(tc, x_words, x_scales, w1, gate, offs, cen, 
 
         def term(b, t, v0, v1):
             part = keep.tile([P, v1 - v0], F32, name=f"part{b}_{t}_{v0}")
-            nc.vector.tensor_tensor(
-                part[:], y[b][:].indirect(lists[t][:, v0 // LANES : v1 // LANES]), factor[t][:, v0:v1], ALU.mult
-            )
+            factor = gates[v0 // HALF][:, t, :] if t < 2 else own[:, v0:v1]
+            nc.vector.tensor_tensor(part[:], y[b][:].indirect(lists[t][:, v0 // LANES : v1 // LANES]), factor, ALU.mult)
             return part
 
         def banks(numbers, name):

@@ -40,7 +40,7 @@ def tile_picked_grand_relu_p_kernel(tc, x_words, x_scales, w1, gate, offs, cen, 
         w_raw = keep.tile([P, PACK, N], F32, name="w_raw")
 
         nc.vector.memset(scale_tab[:FIRST, :].bitcast(I32), 0)
-        nc.sync.dma_start(scale_tab[FIRST:, :].bitcast(I32), x_scales[0].bitcast(I32))
+        nc.scalar.dma_start(scale_tab[FIRST:, :].bitcast(I32), x_scales[0].bitcast(I32))
         nc.sync.dma_start(offs_t[:], offs)
         nc.sync.dma_start(word_tab[:], x_words[0].rearrange("p n t -> p (n t)").bitcast(I32))
         nc.sync.dma_start(cen_t[:], cen)
@@ -93,7 +93,7 @@ def tile_picked_grand_relu_p_kernel(tc, x_words, x_scales, w1, gate, offs, cen, 
         minus_own = keep.tile([P, V], F32, name="minus_own", tag="word_tab", align_bytes=64)
         own = keep.tile([P, V], F32, name="own", tag="w_codes0", align_bytes=64)
 
-        y = [keep.tile([P, S], F32, name=f"y{b}") for b in range(N // P)]
+        y = [keep.tile([P, S], F32, name="y0")]
 
         def product(b, spans, bank, on_vector=False):
             a0, z0 = spans[0][0], spans[-1][1]
@@ -116,7 +116,7 @@ def tile_picked_grand_relu_p_kernel(tc, x_words, x_scales, w1, gate, offs, cen, 
 
         product(0, [(0, 256)], 0)
         product(0, [(256, 512)], 1)
-        product(0, [(512, 768)], 2, True)
+        product(0, [(512, 768)], 2)
         product(0, [(768, 896)], 5)
         product(0, [(896, 1024)], 6, True)
         for h in range(2):
@@ -124,6 +124,7 @@ def tile_picked_grand_relu_p_kernel(tc, x_words, x_scales, w1, gate, offs, cen, 
                 minus_own[:, h * HALF : (h + 1) * HALF], gates[h][:, 0, :], 1.0, gates[h][:, 1, :], ALU.subtract, ALU.add
             )
         nc.scalar.mul(own[:], minus_own[:], -1.0)
+        y.append(keep.tile([P, S], F32, name="y1", tag="word_tab", align_bytes=64))
         product(1, [(0, 512)], 3)
         product(1, [(512, 768), (768, 1024)], 4)
 

@@ -47,9 +47,8 @@ def tile_picked_grand_relu_p_kernel(tc, x_words, x_scales, w1, gate, offs, cen, 
         nc.sync.dma_start(pos1_t[:], pos1)
         nc.sync.dma_start(pos2_t[:], pos2)
         nc.sync.dma_start(w_raw[:], w1.rearrange("(p j) m -> p j m", j=PACK))
-        gate_rows = gate.rearrange("d p v -> p d v")
-        gates = [keep.tile([P, 2, HALF], F32, name="gates0")]
-        nc.sync.dma_start(gates[0][:], gate_rows[:, :, :HALF])
+        gates = [keep.tile([P, V], F32, name="gate0")]
+        nc.sync.dma_start(gates[0][:], gate[0])
 
         ident = keep.tile([P, P], F32, name="ident")
         make_identity(nc, ident[:])
@@ -60,8 +59,8 @@ def tile_picked_grand_relu_p_kernel(tc, x_words, x_scales, w1, gate, offs, cen, 
         for r in range(PACK):
             nc.sync.dma_start(x_scale[r:P:QUAD, :].bitcast(I32), picked[FIRST + r : P : PACK, :].bitcast(I32))
 
-        gates.append(keep.tile([P, 2, HALF], F32, name="gates1", tag="scale_tab", align_bytes=64))
-        nc.sync.dma_start(gates[1][:], gate_rows[:, :, HALF:])
+        gates.append(keep.tile([P, V], F32, name="gate1", tag="scale_tab", align_bytes=64))
+        nc.sync.dma_start(gates[1][:], gate[1])
 
         grouped, w_codes, w_scale = [], [], []
 
@@ -73,8 +72,8 @@ def tile_picked_grand_relu_p_kernel(tc, x_words, x_scales, w1, gate, offs, cen, 
             )
 
         def quantise(b):
-            w_codes.append(keep.tile([P, P], U32, name=f"w_codes{b}", tag=f"w_codes{b}", align_bytes=64))
-            w_scale.append(keep.tile([P, P], U8, name=f"w_scale{b}", align_bytes=64))
+            w_codes.append(keep.tile([P, P], U32, name=f"w_codes{b}", tag="w_codes", align_bytes=64))
+            w_scale.append(keep.tile([P, P], U8, name=f"w_scale{b}", tag=f"w_scale{b}", align_bytes=64))
             nc.vector.quantize_mx(
                 out=w_codes[b][:].bitcast(FP8X4),
                 scales=w_scale[b][:],
@@ -88,10 +87,9 @@ def tile_picked_grand_relu_p_kernel(tc, x_words, x_scales, w1, gate, offs, cen, 
         for a, z, tag in ((0, CUT, "x_codes0"), (CUT, S, "grouped0")):
             x_codes.append(keep.tile([P, z - a], U32, name=f"x_codes{a}", tag=tag, align_bytes=64))
             nc.vector.tensor_copy(x_codes[-1][:], word_tab[:].bitcast(U32).indirect(offs_t[:, a // LANES : z // LANES]))
-        quantise(1)
 
         minus_own = keep.tile([P, V], F32, name="minus_own", tag="word_tab", align_bytes=64)
-        own = keep.tile([P, V], F32, name="own", tag="w_codes0", align_bytes=64)
+        own = keep.tile([P, V], F32, name="own", tag="w_scale0", align_bytes=64)
 
         y = [keep.tile([P, S], F32, name="y0")]
 
@@ -117,12 +115,10 @@ def tile_picked_grand_relu_p_kernel(tc, x_words, x_scales, w1, gate, offs, cen, 
         product(0, [(0, 256)], 0)
         product(0, [(256, 512)], 1)
         product(0, [(512, 768)], 2)
-        product(0, [(768, 896)], 5)
-        product(0, [(896, 1024)], 6, True)
-        for h in range(2):
-            nc.vector.scalar_tensor_tensor(
-                minus_own[:, h * HALF : (h + 1) * HALF], gates[h][:, 0, :], 1.0, gates[h][:, 1, :], ALU.subtract, ALU.add
-            )
+        product(0, [(768, 896)], 5, True)
+        product(0, [(896, 1024)], 6)
+        quantise(1)
+        nc.vector.scalar_tensor_tensor(minus_own[:], gates[0][:], 1.0, gates[1][:], ALU.subtract, ALU.add)
         nc.scalar.mul(own[:], minus_own[:], -1.0)
         y.append(keep.tile([P, S], F32, name="y1", tag="word_tab", align_bytes=64))
         product(1, [(0, 512)], 3)
@@ -132,7 +128,7 @@ def tile_picked_grand_relu_p_kernel(tc, x_words, x_scales, w1, gate, offs, cen, 
 
         def term(b, t, v0, v1):
             part = keep.tile([P, v1 - v0], F32, name=f"part{b}_{t}_{v0}")
-            factor = gates[v0 // HALF][:, t, :] if t < 2 else own[:, v0:v1]
+            factor = (gates + [own])[t][:, v0:v1]
             nc.vector.tensor_tensor(part[:], y[b][:].indirect(lists[t][:, v0 // LANES : v1 // LANES]), factor, ALU.mult)
             return part
 
@@ -157,9 +153,10 @@ def tile_picked_grand_relu_p_kernel(tc, x_words, x_scales, w1, gate, offs, cen, 
 
         there0 = banks((7, 0, 1, 2), "0")
         res0 = keep.tile([P, V], F32, name="res0")
+        for t in range(2):
+            turn_in(there0, term(0, t, 0, V), t == 0, False)
         for h in range(2):
-            for t in range(3):
-                turn_in(there0[2 * h : 2 * h + 2], term(0, t, h * 256, (h + 1) * 256), t == 0, t == 2)
+            turn_in(there0[2 * h : 2 * h + 2], term(0, 2, h * 256, (h + 1) * 256), False, True)
             turn_back(there0[2 * h : 2 * h + 2], 5 + h, res0[:, h * 256 : (h + 1) * 256], f"0_{h}")
         nc.scalar.dma_start(out[:P, :], res0[:])
         there1 = banks((3, 4), "1")

@@ -20,8 +20,8 @@ P = 128
 PACK = 4
 LANES = 16
 QUAD = 32
-CUT = 768
 HALF = V // 2
+BLOCKS = V // P
 FIRST = P - K // 32
 
 
@@ -35,20 +35,19 @@ def tile_picked_grand_relu_p_kernel(tc, x_words, x_scales, w1, gate, offs, cen, 
         cen_t = keep.tile([P, V // LANES], U16, name="cen_t")
         pos1_t = keep.tile([P, V // LANES], U16, name="pos1_t")
         pos2_t = keep.tile([P, V // LANES], U16, name="pos2_t")
-        scale_tab = keep.tile([P, T], U8, name="scale_tab", tag="scale_tab", align_bytes=64)
-        word_tab = keep.tile([P, T], I32, name="word_tab", tag="word_tab", align_bytes=64)
+        scale_tab = keep.tile([P, T], U8, name="scale_tab", align_bytes=64)
+        word_tab = keep.tile([P, T], I32, name="word_tab", align_bytes=64)
         w_raw = keep.tile([P, PACK, N], F32, name="w_raw")
+        gate_rows = keep.tile([P, P], F32, name="gate_rows")
 
         nc.vector.memset(scale_tab[:FIRST, :].bitcast(I32), 0)
         nc.scalar.dma_start(scale_tab[FIRST:, :].bitcast(I32), x_scales[0].bitcast(I32))
         nc.sync.dma_start(offs_t[:], offs)
+        nc.sync.dma_start(gate_rows[:], gate[:, :LANES, :].rearrange("d r (b c) -> d (r b) c", c=P))
         nc.sync.dma_start(word_tab[:], x_words[0].rearrange("p n t -> p (n t)").bitcast(I32))
+        nc.sync.dma_start(w_raw[:], w1.rearrange("(p j) m -> p j m", j=PACK))
         nc.sync.dma_start(cen_t[:], cen)
         nc.sync.dma_start(pos1_t[:], pos1)
-        nc.sync.dma_start(pos2_t[:], pos2)
-        nc.sync.dma_start(w_raw[:], w1.rearrange("(p j) m -> p j m", j=PACK))
-        gates = [keep.tile([P, V], F32, name="gate0")]
-        nc.sync.dma_start(gates[0][:], gate[0])
 
         ident = keep.tile([P, P], F32, name="ident")
         make_identity(nc, ident[:])
@@ -58,118 +57,147 @@ def tile_picked_grand_relu_p_kernel(tc, x_words, x_scales, w1, gate, offs, cen, 
         x_scale = keep.tile([P, S], U8, name="x_scale", align_bytes=64)
         for r in range(PACK):
             nc.sync.dma_start(x_scale[r:P:QUAD, :].bitcast(I32), picked[FIRST + r : P : PACK, :].bitcast(I32))
+        nc.sync.dma_start(pos2_t[:], pos2)
+        x_codes = keep.tile([P, S], U32, name="x_codes", align_bytes=64)
+        nc.vector.tensor_copy(x_codes[:], word_tab[:].bitcast(U32).indirect(offs_t[:]))
 
-        gates.append(keep.tile([P, V], F32, name="gate1", tag="scale_tab", align_bytes=64))
-        nc.sync.dma_start(gates[1][:], gate[1])
+        turned = psum.tile([P, P], F32, name="turned", tag="bank7")
+        nc.tensor.transpose(turned[:], gate_rows[:], ident[:])
+        cols = keep.tile([P, 3, BLOCKS], F32, name="cols", tag="grouped0", align_bytes=64)
+        late = keep.tile([P, 2, 2], F32, name="late")
+        nc.scalar.copy(cols[:, :2, :], turned[:].rearrange("p (d q) -> p d q", d=2)[:, :, :BLOCKS])
+        rest = keep.tile([P, BLOCKS], F32, name="rest")
+        nc.scalar.activation(rest[:], turned[:, :BLOCKS], ACT.Identity, bias=1.0, scale=-1.0)
+        for j in range(BLOCKS):
+            own = cols[:, 2, j : j + 1] if j < 2 else late[:, 0, j - 2 : j - 1]
+            nc.scalar.activation(own, cols[:, 1, j : j + 1], ACT.Identity, bias=rest[:, j : j + 1], scale=-1.0)
+        nc.scalar.copy(late[:, 1, :], cols[:, 0, 2:])
 
-        grouped, w_codes, w_scale = [], [], []
+        def spread(name, picks, bank):
+            wide = psum.tile([P, len(picks) * P], F32, name=f"wide_{name}", tag=f"bank{bank}")
+            for i, (d, j) in enumerate(picks):
+                nc.tensor.transpose(wide[:, i * P : (i + 1) * P], cols[:, d, j : j + 1].to_broadcast([P, P]), ident[:])
+            factor = keep.tile([P, len(picks) * P], F32, name=f"factor_{name}")
+            nc.scalar.copy(factor[:], wide[:])
+            return factor
 
-        def cast(b):
-            grouped.append(keep.tile([P, P, PACK], BF16, name=f"grouped{b}", tag=f"grouped{b}", align_bytes=64))
+        first = spread("first", [(0, 0), (0, 1), (2, 0), (2, 1)], 5)
+        second = spread("second", [(1, j) for j in range(BLOCKS)], 6)
+
+        w_codes, w_scale = [], []
+        both = keep.tile([P, N * PACK], BF16, name="both", tag="grouped0", align_bytes=64)
+        for b in range(2):
+            grouped = both[:, b * P * PACK : (b + 1) * P * PACK]
             nc.scalar.copy(
-                grouped[b][:].rearrange("p (c i) j -> p c j i", i=PACK),
+                grouped.rearrange("p (m j) -> p m j", j=PACK).rearrange("p (c i) j -> p c j i", i=PACK),
                 w_raw[:, :, b * P : (b + 1) * P].rearrange("p j (c i) -> p c j i", i=PACK),
             )
-
-        def quantise(b):
-            w_codes.append(keep.tile([P, P], U32, name=f"w_codes{b}", tag="w_codes", align_bytes=64))
-            w_scale.append(keep.tile([P, P], U8, name=f"w_scale{b}", tag=f"w_scale{b}", align_bytes=64))
+            w_codes.append(keep.tile([P, P], U32, name=f"w_codes{b}", align_bytes=64))
+            w_scale.append(keep.tile([P, P], U8, name=f"w_scale{b}", align_bytes=64))
             nc.vector.quantize_mx(
-                out=w_codes[b][:].bitcast(FP8X4),
-                scales=w_scale[b][:],
-                in_=grouped[b][:].rearrange("p m j -> p (m j)"),
+                out=w_codes[b][:].bitcast(FP8X4), scales=w_scale[b][:], in_=grouped
             )
 
-        cast(0)
-        quantise(0)
-        cast(1)
-        x_codes = []
-        for a, z, tag in ((0, CUT, "x_codes0"), (CUT, S, "grouped0")):
-            x_codes.append(keep.tile([P, z - a], U32, name=f"x_codes{a}", tag=tag, align_bytes=64))
-            nc.vector.tensor_copy(x_codes[-1][:], word_tab[:].bitcast(U32).indirect(offs_t[:, a // LANES : z // LANES]))
+        y = [keep.tile([P, S], F32, name=f"y{b}") for b in range(2)]
 
-        minus_own = keep.tile([P, V], F32, name="minus_own", tag="word_tab", align_bytes=64)
-        own = keep.tile([P, V], F32, name="own", tag="w_scale0", align_bytes=64)
-
-        y = [keep.tile([P, S], F32, name="y0")]
-
-        def product(b, spans, bank, on_vector=False):
-            a0, z0 = spans[0][0], spans[-1][1]
-            acc = psum.tile([P, z0 - a0], F32, name=f"acc{b}_{a0}", tag=f"bank{bank}")
-            for a, z in spans:
-                i, off = divmod(a, CUT)
-                nc.tensor.matmul_mx(
-                    out=acc[:, a - a0 : z - a0],
-                    lhsT=w_codes[b][:].bitcast(FP8X4),
-                    lhsT_scale=w_scale[b][:],
-                    rhs=x_codes[i][:, off : off + z - a].bitcast(FP8X4),
-                    rhs_scale=x_scale[:, a:z],
-                    start=True,
-                    stop=True,
-                )
+        def product(b, a, z, bank, on_vector=False):
+            acc = psum.tile([P, z - a], F32, name=f"acc{b}_{a}", tag=f"bank{bank}")
+            nc.tensor.matmul_mx(
+                out=acc[:],
+                lhsT=w_codes[b][:].bitcast(FP8X4),
+                lhsT_scale=w_scale[b][:],
+                rhs=x_codes[:, a:z].bitcast(FP8X4),
+                rhs_scale=x_scale[:, a:z],
+                start=True,
+                stop=True,
+            )
             if on_vector:
-                nc.vector.tensor_scalar_max(y[b][:, a0:z0], acc[:], 0.0)
+                nc.vector.tensor_scalar_max(y[b][:, a:z], acc[:], 0.0)
             else:
-                nc.scalar.activation(y[b][:, a0:z0], acc[:], ACT.Relu)
+                nc.scalar.activation(y[b][:, a:z], acc[:], ACT.Relu)
 
-        product(0, [(0, 256)], 0)
-        product(0, [(256, 512)], 1)
-        product(0, [(512, 768)], 2)
-        product(0, [(768, 896)], 5, True)
-        product(0, [(896, 1024)], 6)
-        quantise(1)
-        nc.vector.scalar_tensor_tensor(minus_own[:], gates[0][:], 1.0, gates[1][:], ALU.subtract, ALU.add)
-        nc.scalar.mul(own[:], minus_own[:], -1.0)
-        y.append(keep.tile([P, S], F32, name="y1", tag="word_tab", align_bytes=64))
-        product(1, [(0, 512)], 3)
-        product(1, [(512, 768), (768, 1024)], 4)
+        for i in range(4):
+            product(0, i * 256, (i + 1) * 256, i, i % 2 == 0)
+        product(1, 0, 512, 4, True)
 
-        lists = [pos1_t, pos2_t, cen_t]
+        def fused(part, b, lst, factor, v0, v1):
+            nc.vector.tensor_tensor(part, y[b][:].indirect(lst[:, v0 // LANES : v1 // LANES]), factor, ALU.mult)
 
-        def term(b, t, v0, v1):
-            part = keep.tile([P, v1 - v0], F32, name=f"part{b}_{t}_{v0}")
-            factor = (gates + [own])[t][:, v0:v1]
-            nc.vector.tensor_tensor(part[:], y[b][:].indirect(lists[t][:, v0 // LANES : v1 // LANES]), factor, ALU.mult)
+        def plain(b, lst, name):
+            part = keep.tile([P, HALF], F32, name=f"plain{name}{b}")
+            nc.scalar.activation(part[:], y[b][:].indirect(lst[:, HALF // LANES :]), ACT.Copy)
             return part
 
-        def banks(numbers, name):
-            return [psum.tile([P, P], F32, name=f"there{name}_{n}", tag=f"bank{n}") for n in numbers]
+        def summed_band(b):
+            theres = [psum.tile([P, P], F32, name=f"there{b}_{i}", tag=f"bank{2 * b + i}") for i in range(2)]
+            terms = ((pos1_t, first[:, :HALF]), (pos2_t, second[:, :HALF]), (cen_t, first[:, HALF:]))
+            for t, (lst, factor) in enumerate(terms):
+                part = keep.tile([P, HALF], F32, name=f"part{b}_{t}")
+                fused(part[:], b, lst, factor, 0, HALF)
+                for i in range(2):
+                    nc.tensor.matmul(
+                        theres[i][:], part[:, i * P : (i + 1) * P], ident[:], start=t == 0, stop=t == 2, is_transpose=True
+                    )
+            return theres
 
-        def turn_in(theres, part, first, last):
-            for i, there in enumerate(theres):
-                nc.tensor.matmul(
-                    there[:], part[:, i * P : (i + 1) * P], ident[:], start=first, stop=last, is_transpose=True
-                )
+        def turn_back(b, theres):
+            summed = keep.tile([P, HALF], F32, name=f"summed{b}")
+            for i in range(2):
+                nc.scalar.copy(summed[:, i * P : (i + 1) * P], theres[i][:])
+            back = psum.tile([P, HALF], F32, name=f"back{b}", tag=f"bank{4 + b}")
+            for i in range(2):
+                nc.tensor.transpose(back[:, i * P : (i + 1) * P], summed[:, i * P : (i + 1) * P], ident[:])
+            return back
 
-        def turn_back(theres, number, res, name):
-            width = len(theres) * P
-            summed = keep.tile([P, width], F32, name=f"summed{name}")
-            for i, there in enumerate(theres):
-                nc.scalar.copy(summed[:, i * P : (i + 1) * P], there[:])
-            back = psum.tile([P, width], F32, name=f"back{name}", tag=f"bank{number}")
-            for c in range(0, width, P):
-                nc.tensor.transpose(back[:, c : c + P], summed[:, c : c + P], ident[:])
-            nc.scalar.copy(res, back[:])
+        def leave(b, back):
+            res = keep.tile([P, HALF], F32, name=f"res{b}")
+            nc.scalar.copy(res[:], back[:])
+            nc.scalar.dma_start(out[b * P : (b + 1) * P, :HALF], res[:])
 
-        there0 = banks((7, 0, 1, 2), "0")
-        res0 = keep.tile([P, V], F32, name="res0")
-        for t in range(2):
-            turn_in(there0, term(0, t, 0, V), t == 0, False)
-        for h in range(2):
-            turn_in(there0[2 * h : 2 * h + 2], term(0, 2, h * 256, (h + 1) * 256), False, True)
-            turn_back(there0[2 * h : 2 * h + 2], 5 + h, res0[:, h * 256 : (h + 1) * 256], f"0_{h}")
-        nc.scalar.dma_start(out[:P, :], res0[:])
-        there1 = banks((3, 4), "1")
-        for t in range(3):
-            turn_in(there1, term(1, t, 0, 256), t == 0, t == 2)
-        res1 = keep.tile([P, 256], F32, name="res1")
-        turn_back(there1, 7, res1[:], "1")
-        nc.scalar.dma_start(out[P:, :256], res1[:])
-        parts = [term(1, t, 256, 512) for t in range(3)]
-        pairs = [keep.tile([P, P], F32, name=f"pair{h}") for h in range(2)]
-        for h in range(2):
-            nc.vector.tensor_tensor(pairs[h][:], parts[0][:, h * P : (h + 1) * P], parts[1][:, h * P : (h + 1) * P], ALU.add)
-        for h in range(2):
-            res = keep.tile([P, P], F32, name=f"last{h}")
-            nc.vector.tensor_tensor(res[:], pairs[h][:], parts[2][:, h * P : (h + 1) * P], ALU.add)
-            nc.sync.dma_start(out[P:, 256 + h * P : 256 + (h + 1) * P], res[:])
+        def turn_in(there, b, part):
+            for i in range(2):
+                nc.tensor.transpose(there[:, i, b * P : (b + 1) * P], part[:, i * P : (i + 1) * P], ident[:])
+
+        def scale(there, d, i):
+            scaled = keep.tile([P, N], F32, name=f"scaled{d}_{i}")
+            nc.scalar.activation(scaled[:], there[:, i, :], ACT.Copy, scale=late[:, d, i : i + 1])
+            return scaled
+
+        def pair_up(i, scaled):
+            pair = psum.tile([P, 2, P], F32, name=f"pair{i}", tag=f"bank{2 * i}")
+            for b in range(2):
+                for t in range(2):
+                    nc.tensor.matmul(
+                        pair[:, b, :],
+                        scaled[t][:, b * P : (b + 1) * P],
+                        ident[:],
+                        start=t == 0,
+                        stop=t == 1,
+                        is_transpose=True,
+                    )
+            return pair
+
+        centre = psum.tile([P, 2, N], F32, name="centre", tag="bank6")
+        neighbour = psum.tile([P, 2, N], F32, name="neighbour", tag="bank7")
+        turn_in(centre, 0, plain(0, cen_t, "c"))
+        product(1, 512, 1024, 5)
+        turn_in(neighbour, 0, plain(0, pos1_t, "n"))
+        there0 = summed_band(0)
+        turn_in(centre, 1, plain(1, cen_t, "c"))
+        turn_in(neighbour, 1, plain(1, pos1_t, "n"))
+        back0 = turn_back(0, there0)
+        there1 = summed_band(1)
+        pairs = [pair_up(0, [scale(centre, 0, 0), scale(neighbour, 1, 0)])]
+        last = keep.tile([P, 2, HALF], F32, name="last")
+        for b in range(2):
+            fused(last[:, b, :], b, pos2_t, second[:, HALF:], HALF, V)
+        scaled_c = scale(centre, 0, 1)
+        back1 = turn_back(1, there1)
+        pairs.append(pair_up(1, [scaled_c, scale(neighbour, 1, 1)]))
+        leave(0, back0)
+        leave(1, back1)
+        for i in range(2):
+            res = keep.tile([P, 2, P], F32, name=f"end{i}")
+            nc.vector.tensor_tensor(res[:], pairs[i][:], last[:, :, i * P : (i + 1) * P], ALU.add)
+            a = HALF + i * P
+            nc.sync.dma_start(out[:, a : a + P].rearrange("(b p) v -> p b v", p=P), res[:])

@@ -43,7 +43,8 @@ def tile_picked_grand_relu_p_kernel(tc, x_words, x_scales, w1, gate, offs, cen, 
         nc.vector.memset(scale_tab[:FIRST, :].bitcast(I32), 0)
         nc.scalar.dma_start(scale_tab[FIRST:, :].bitcast(I32), x_scales[0].bitcast(I32))
         nc.sync.dma_start(offs_t[:], offs)
-        nc.sync.dma_start(gate_rows[:], gate[:, :LANES, :].rearrange("d r (b c) -> d (r b) c", c=P))
+        for d in range(2):
+            nc.sync.dma_start(gate_rows[d * 64 : (d + 1) * 64, :], gate[d, :LANES, :].rearrange("r (b c) -> (r b) c", c=P))
         nc.sync.dma_start(word_tab[:], x_words[0].rearrange("p n t -> p (n t)").bitcast(I32))
         nc.sync.dma_start(w_raw[:], w1.rearrange("(p j) m -> p j m", j=PACK))
         nc.sync.dma_start(cen_t[:], cen)

@@ -23,12 +23,15 @@ QUAD = 32
 HALF = V // 2
 BLOCKS = V // P
 FIRST = P - K // 32
+CUT = 768
+BAND_BYTES = P * PACK * 2
 
 
 def tile_picked_grand_relu_p_kernel(tc, x_words, x_scales, w1, gate, offs, cen, pos1, pos2, out):
     nc = tc.nc
     with ExitStack() as ctx:
         keep = ctx.enter_context(tc.tile_pool(name="keep", bufs=1))
+        turns = ctx.enter_context(tc.tile_pool(name="turns", bufs=1))
         psum = ctx.enter_context(tc.psum_pool(name="psum", bufs=1))
 
         offs_t = keep.tile([P, S // LANES], U16, name="offs_t")
@@ -44,11 +47,10 @@ def tile_picked_grand_relu_p_kernel(tc, x_words, x_scales, w1, gate, offs, cen, 
         nc.scalar.dma_start(scale_tab[FIRST:, :].bitcast(I32), x_scales[0].bitcast(I32))
         nc.sync.dma_start(offs_t[:], offs)
         for d in range(2):
-            nc.sync.dma_start(gate_rows[d * 64 : (d + 1) * 64, :], gate[d, :LANES, :].rearrange("r (b c) -> (r b) c", c=P))
+            nc.scalar.dma_start(gate_rows[d * 64 : (d + 1) * 64, :], gate[d, :LANES, :].rearrange("r (b c) -> (r b) c", c=P))
         nc.sync.dma_start(word_tab[:], x_words[0].rearrange("p n t -> p (n t)").bitcast(I32))
         nc.sync.dma_start(w_raw[:], w1.rearrange("(p j) m -> p j m", j=PACK))
         nc.sync.dma_start(cen_t[:], cen)
-        nc.sync.dma_start(pos1_t[:], pos1)
 
         ident = keep.tile([P, P], F32, name="ident")
         make_identity(nc, ident[:])
@@ -58,13 +60,14 @@ def tile_picked_grand_relu_p_kernel(tc, x_words, x_scales, w1, gate, offs, cen, 
         x_scale = keep.tile([P, S], U8, name="x_scale", align_bytes=64)
         for r in range(PACK):
             nc.sync.dma_start(x_scale[r:P:QUAD, :].bitcast(I32), picked[FIRST + r : P : PACK, :].bitcast(I32))
+        nc.sync.dma_start(pos1_t[:], pos1)
         nc.sync.dma_start(pos2_t[:], pos2)
-        x_codes = keep.tile([P, S], U32, name="x_codes", align_bytes=64)
-        nc.vector.tensor_copy(x_codes[:], word_tab[:].bitcast(U32).indirect(offs_t[:]))
+        x_codes = [keep.tile([P, CUT], U32, name="x_codes0", align_bytes=64)]
+        nc.vector.tensor_copy(x_codes[0][:], word_tab[:].bitcast(U32).indirect(offs_t[:, : CUT // LANES]))
 
         turned = psum.tile([P, P], F32, name="turned", tag="bank7")
         nc.tensor.transpose(turned[:], gate_rows[:], ident[:])
-        cols = keep.tile([P, 3, BLOCKS], F32, name="cols", tag="grouped0", align_bytes=64)
+        cols = turns.tile([P, 3, BLOCKS], F32, name="cols", offset=BAND_BYTES - 32)
         late = keep.tile([P, 2, 2], F32, name="late")
         nc.scalar.copy(cols[:, :2, :], turned[:].rearrange("p (d q) -> p d q", d=2)[:, :, :BLOCKS])
         rest = keep.tile([P, BLOCKS], F32, name="rest")
@@ -86,39 +89,47 @@ def tile_picked_grand_relu_p_kernel(tc, x_words, x_scales, w1, gate, offs, cen, 
         second = spread("second", [(1, j) for j in range(BLOCKS)], 6)
 
         w_codes, w_scale = [], []
-        both = keep.tile([P, N * PACK], BF16, name="both", tag="grouped0", align_bytes=64)
         for b in range(2):
-            grouped = both[:, b * P * PACK : (b + 1) * P * PACK]
+            grouped = turns.tile([P, P, PACK], BF16, name=f"grouped{b}", offset=b * BAND_BYTES, align_bytes=64)
             nc.scalar.copy(
-                grouped.rearrange("p (m j) -> p m j", j=PACK).rearrange("p (c i) j -> p c j i", i=PACK),
+                grouped[:].rearrange("p (c i) j -> p c j i", i=PACK),
                 w_raw[:, :, b * P : (b + 1) * P].rearrange("p j (c i) -> p c j i", i=PACK),
             )
             w_codes.append(keep.tile([P, P], U32, name=f"w_codes{b}", align_bytes=64))
             w_scale.append(keep.tile([P, P], U8, name=f"w_scale{b}", align_bytes=64))
             nc.vector.quantize_mx(
-                out=w_codes[b][:].bitcast(FP8X4), scales=w_scale[b][:], in_=grouped
+                out=w_codes[b][:].bitcast(FP8X4), scales=w_scale[b][:], in_=grouped[:].rearrange("p m j -> p (m j)")
             )
+            if b == 0:
+                x_codes.append(turns.tile([P, S - CUT], U32, name="x_codes1", offset=0, align_bytes=64))
+                nc.vector.tensor_copy(x_codes[1][:], word_tab[:].bitcast(U32).indirect(offs_t[:, CUT // LANES :]))
 
         y = [keep.tile([P, S], F32, name=f"y{b}") for b in range(2)]
 
-        def product(b, a, z, bank, on_vector=False):
-            acc = psum.tile([P, z - a], F32, name=f"acc{b}_{a}", tag=f"bank{bank}")
+        def product(b, a0, z0, bank, on_vector=False):
+            acc = psum.tile([P, z0 - a0], F32, name=f"acc{b}_{a0}", tag=f"bank{bank}")
+            for a, z in ((a0, CUT), (CUT, z0)) if a0 < CUT < z0 else ((a0, z0),):
+                one_pass(acc[:, a - a0 : z - a0], b, a, z)
+            if on_vector:
+                nc.vector.tensor_scalar_max(y[b][:, a0:z0], acc[:], 0.0)
+            else:
+                nc.scalar.activation(y[b][:, a0:z0], acc[:], ACT.Relu)
+
+        def one_pass(acc, b, a, z):
             nc.tensor.matmul_mx(
-                out=acc[:],
+                out=acc,
                 lhsT=w_codes[b][:].bitcast(FP8X4),
                 lhsT_scale=w_scale[b][:],
-                rhs=x_codes[:, a:z].bitcast(FP8X4),
+                rhs=x_codes[a // CUT][:, a % CUT : a % CUT + z - a].bitcast(FP8X4),
                 rhs_scale=x_scale[:, a:z],
                 start=True,
                 stop=True,
             )
-            if on_vector:
-                nc.vector.tensor_scalar_max(y[b][:, a:z], acc[:], 0.0)
-            else:
-                nc.scalar.activation(y[b][:, a:z], acc[:], ACT.Relu)
 
-        for i in range(4):
+        for i in range(3):
             product(0, i * 256, (i + 1) * 256, i, i % 2 == 0)
+        product(0, 768, 896, 3)
+        product(0, 896, 1024, 7, True)
         product(1, 0, 512, 4, True)
 
         def fused(part, b, lst, factor, v0, v1):

@@ -38,59 +38,46 @@ def tile_picked_grand_relu_p_kernel(tc, x_words, x_scales, w1, gate, offs, cen, 
         cen_t = keep.tile([P, V // LANES], U16, name="cen_t")
         pos1_t = keep.tile([P, V // LANES], U16, name="pos1_t")
         pos2_t = keep.tile([P, V // LANES], U16, name="pos2_t")
-        scale_tab = keep.tile([P, T], U8, name="scale_tab", align_bytes=64)
+        scale_tab = turns.tile([P, T], U8, name="scale_tab", offset=0, align_bytes=64)
         word_tab = keep.tile([P, T], I32, name="word_tab", align_bytes=64)
         w_raw = keep.tile([P, PACK, N], F32, name="w_raw")
-        gate_rows = keep.tile([P, P], F32, name="gate_rows")
+        first = keep.tile([P, 2, HALF], F32, name="first")
 
         nc.vector.memset(scale_tab[:FIRST, :].bitcast(I32), 0)
         nc.scalar.dma_start(scale_tab[FIRST:, :].bitcast(I32), x_scales[0].bitcast(I32))
         nc.sync.dma_start(offs_t[:], offs)
-        for d in range(2):
-            nc.scalar.dma_start(gate_rows[d * 64 : (d + 1) * 64, :], gate[d, :LANES, :].rearrange("r (b c) -> (r b) c", c=P))
         nc.sync.dma_start(word_tab[:], x_words[0].rearrange("p n t -> p (n t)").bitcast(I32))
-        nc.sync.dma_start(w_raw[:], w1.rearrange("(p j) m -> p j m", j=PACK))
         nc.sync.dma_start(cen_t[:], cen)
+        nc.sync.dma_start(pos1_t[:], pos1)
+        nc.sync.dma_start(pos2_t[:], pos2)
+        nc.sync.dma_start(w_raw[:], w1.rearrange("(p j) m -> p j m", j=PACK))
+        nc.sync.dma_start(first[:], gate[:, :, :HALF].rearrange("d p v -> p d v"))
 
         ident = keep.tile([P, P], F32, name="ident")
         make_identity(nc, ident[:])
 
-        picked = keep.tile([P, S], U8, name="picked", align_bytes=64)
+        picked = keep.tile([P, S], U8, name="picked", tag="picked", align_bytes=64)
         nc.vector.tensor_copy(picked[:], scale_tab[:].indirect(offs_t[:]))
         x_scale = keep.tile([P, S], U8, name="x_scale", align_bytes=64)
         for r in range(PACK):
             nc.sync.dma_start(x_scale[r:P:QUAD, :].bitcast(I32), picked[FIRST + r : P : PACK, :].bitcast(I32))
-        nc.sync.dma_start(pos1_t[:], pos1)
-        nc.sync.dma_start(pos2_t[:], pos2)
         x_codes = [keep.tile([P, CUT], U32, name="x_codes0", align_bytes=64)]
         nc.vector.tensor_copy(x_codes[0][:], word_tab[:].bitcast(U32).indirect(offs_t[:, : CUT // LANES]))
 
-        turned = psum.tile([P, P], F32, name="turned", tag="bank7")
-        nc.tensor.transpose(turned[:], gate_rows[:], ident[:])
-        cols = turns.tile([P, 3, BLOCKS], F32, name="cols", offset=BAND_BYTES - 32)
-        late = keep.tile([P, 2, 2], F32, name="late")
-        nc.scalar.copy(cols[:, :2, :], turned[:].rearrange("p (d q) -> p d q", d=2)[:, :, :BLOCKS])
-        rest = keep.tile([P, BLOCKS], F32, name="rest")
-        nc.scalar.activation(rest[:], turned[:, :BLOCKS], ACT.Identity, bias=1.0, scale=-1.0)
-        for j in range(BLOCKS):
-            own = cols[:, 2, j : j + 1] if j < 2 else late[:, 0, j - 2 : j - 1]
-            nc.scalar.activation(own, cols[:, 1, j : j + 1], ACT.Identity, bias=rest[:, j : j + 1], scale=-1.0)
-        nc.scalar.copy(late[:, 1, :], cols[:, 0, 2:])
-
-        def spread(name, picks, bank):
-            wide = psum.tile([P, len(picks) * P], F32, name=f"wide_{name}", tag=f"bank{bank}")
-            for i, (d, j) in enumerate(picks):
-                nc.tensor.transpose(wide[:, i * P : (i + 1) * P], cols[:, d, j : j + 1].to_broadcast([P, P]), ident[:])
-            factor = keep.tile([P, len(picks) * P], F32, name=f"factor_{name}")
-            nc.scalar.copy(factor[:], wide[:])
-            return factor
-
-        first = spread("first", [(0, 0), (0, 1), (2, 0), (2, 1)], 5)
-        second = spread("second", [(1, j) for j in range(BLOCKS)], 6)
+        second = turns.tile([P, HALF], F32, name="second", offset=0)
+        nc.sync.dma_start(second[:], gate[1, :, HALF:])
+        cols = keep.tile([P, 2, 8], F32, name="cols", tag="picked", align_bytes=64)
+        with nc.allow_non_contiguous_dma(reason="one gate value a partition"):
+            for d in range(2):
+                nc.sync.dma_start(cols[:, d, :2], gate[d, 0, HALF:].rearrange("(i p) -> p i", p=P))
+        rest = keep.tile([P, 2], F32, name="rest")
+        own_cols = keep.tile([P, 2], F32, name="own_cols")
+        nc.gpsimd.tensor_scalar(rest[:], cols[:, 0, :2], -1.0, 1.0, ALU.mult, ALU.add)
+        nc.gpsimd.tensor_tensor(own_cols[:], rest[:], cols[:, 1, :2], ALU.subtract)
 
         w_codes, w_scale = [], []
         for b in range(2):
-            grouped = turns.tile([P, P, PACK], BF16, name=f"grouped{b}", offset=b * BAND_BYTES, align_bytes=64)
+            grouped = turns.tile([P, P, PACK], BF16, name=f"grouped{b}", offset=T + b * BAND_BYTES, align_bytes=64)
             nc.scalar.copy(
                 grouped[:].rearrange("p (c i) j -> p c j i", i=PACK),
                 w_raw[:, :, b * P : (b + 1) * P].rearrange("p j (c i) -> p c j i", i=PACK),
@@ -101,8 +88,13 @@ def tile_picked_grand_relu_p_kernel(tc, x_words, x_scales, w1, gate, offs, cen, 
                 out=w_codes[b][:].bitcast(FP8X4), scales=w_scale[b][:], in_=grouped[:].rearrange("p m j -> p (m j)")
             )
             if b == 0:
-                x_codes.append(turns.tile([P, S - CUT], U32, name="x_codes1", offset=0, align_bytes=64))
+                x_codes.append(turns.tile([P, S - CUT], U32, name="x_codes1", offset=T, align_bytes=64))
                 nc.vector.tensor_copy(x_codes[1][:], word_tab[:].bitcast(U32).indirect(offs_t[:, CUT // LANES :]))
+
+        less = keep.tile([P, HALF], F32, name="less")
+        nc.scalar.activation(less[:], first[:, 0, :], ACT.Identity, bias=1.0, scale=-1.0)
+        own = keep.tile([P, HALF], F32, name="own")
+        nc.vector.tensor_tensor(own[:], less[:], first[:, 1, :], ALU.subtract)
 
         y = [keep.tile([P, S], F32, name=f"y{b}") for b in range(2)]
 
@@ -130,7 +122,6 @@ def tile_picked_grand_relu_p_kernel(tc, x_words, x_scales, w1, gate, offs, cen, 
             product(0, i * 256, (i + 1) * 256, i, i % 2 == 0)
         product(0, 768, 896, 3)
         product(0, 896, 1024, 7, True)
-        product(1, 0, 512, 4, True)
 
         def fused(part, b, lst, factor, v0, v1):
             nc.vector.tensor_tensor(part, y[b][:].indirect(lst[:, v0 // LANES : v1 // LANES]), factor, ALU.mult)
@@ -140,76 +131,79 @@ def tile_picked_grand_relu_p_kernel(tc, x_words, x_scales, w1, gate, offs, cen, 
             nc.scalar.activation(part[:], y[b][:].indirect(lst[:, HALF // LANES :]), ACT.Copy)
             return part
 
-        def summed_band(b):
-            theres = [psum.tile([P, P], F32, name=f"there{b}_{i}", tag=f"bank{2 * b + i}") for i in range(2)]
-            terms = ((pos1_t, first[:, :HALF]), (pos2_t, second[:, :HALF]), (cen_t, first[:, HALF:]))
-            for t, (lst, factor) in enumerate(terms):
-                part = keep.tile([P, HALF], F32, name=f"part{b}_{t}")
-                fused(part[:], b, lst, factor, 0, HALF)
+        def turn(acc, part, start, stop):
+            nc.tensor.matmul(acc, part, ident[:], start=start, stop=stop, is_transpose=True)
+
+        def three_terms(b):
+            parts = []
+            for t, (lst, factor) in enumerate(((pos1_t, first[:, 0, :]), (pos2_t, first[:, 1, :]), (cen_t, own[:]))):
+                parts.append(keep.tile([P, HALF], F32, name=f"part{b}_{t}"))
+                fused(parts[t][:], b, lst, factor, 0, HALF)
+            return parts
+
+        def add_up(b, parts, bank):
+            there = psum.tile([P, 2, P], F32, name=f"there{b}", tag=f"bank{bank}")
+            for t, part in enumerate(parts):
                 for i in range(2):
-                    nc.tensor.matmul(
-                        theres[i][:], part[:, i * P : (i + 1) * P], ident[:], start=t == 0, stop=t == 2, is_transpose=True
-                    )
-            return theres
+                    turn(there[:, i, :], part[:, i * P : (i + 1) * P], (t, i) == (0, 0), (t, i) == (2, 1))
+            return there
 
-        def turn_back(b, theres):
-            summed = keep.tile([P, HALF], F32, name=f"summed{b}")
+        def turn_back(b, there):
+            summed = keep.tile([P, 2, P], F32, name=f"summed{b}")
+            nc.scalar.copy(summed[:], there[:])
+            back = psum.tile([P, HALF], F32, name=f"back{b}", tag=f"bank{(7, 4)[b]}")
             for i in range(2):
-                nc.scalar.copy(summed[:, i * P : (i + 1) * P], theres[i][:])
-            back = psum.tile([P, HALF], F32, name=f"back{b}", tag=f"bank{4 + b}")
-            for i in range(2):
-                nc.tensor.transpose(back[:, i * P : (i + 1) * P], summed[:, i * P : (i + 1) * P], ident[:])
+                nc.tensor.transpose(back[:, i * P : (i + 1) * P], summed[:, i, :], ident[:])
             return back
-
-        def leave(b, back):
-            res = keep.tile([P, HALF], F32, name=f"res{b}")
-            nc.scalar.copy(res[:], back[:])
-            nc.scalar.dma_start(out[b * P : (b + 1) * P, :HALF], res[:])
 
         def turn_in(there, b, part):
             for i in range(2):
                 nc.tensor.transpose(there[:, i, b * P : (b + 1) * P], part[:, i * P : (i + 1) * P], ident[:])
 
-        def scale(there, d, i):
+        def scale_back(pair, there, d, i):
             scaled = keep.tile([P, N], F32, name=f"scaled{d}_{i}")
-            nc.scalar.activation(scaled[:], there[:, i, :], ACT.Copy, scale=late[:, d, i : i + 1])
-            return scaled
-
-        def pair_up(i, scaled):
-            pair = psum.tile([P, 2, P], F32, name=f"pair{i}", tag=f"bank{2 * i}")
+            nc.scalar.activation(
+                scaled[:], there[:, i, :], ACT.Copy, scale=(own_cols[:], cols[:, 0, :])[d][:, i : i + 1]
+            )
             for b in range(2):
-                for t in range(2):
-                    nc.tensor.matmul(
-                        pair[:, b, :],
-                        scaled[t][:, b * P : (b + 1) * P],
-                        ident[:],
-                        start=t == 0,
-                        stop=t == 1,
-                        is_transpose=True,
-                    )
-            return pair
+                turn(pair[:, b, :], scaled[:, b * P : (b + 1) * P], (d, b) == (0, 0), (d, b) == (1, 1))
 
-        centre = psum.tile([P, 2, N], F32, name="centre", tag="bank6")
-        neighbour = psum.tile([P, 2, N], F32, name="neighbour", tag="bank7")
-        turn_in(centre, 0, plain(0, cen_t, "c"))
-        product(1, 512, 1024, 5)
-        turn_in(neighbour, 0, plain(0, pos1_t, "n"))
-        there0 = summed_band(0)
+        def finish_first(b, back):
+            res = keep.tile([P, HALF], F32, name=f"res{b}")
+            nc.scalar.copy(res[:], back[:])
+            (nc.sync, nc.scalar)[b].dma_start(out[b * P : (b + 1) * P, :HALF], res[:])
+
+        def finish_second(i, pair):
+            a = HALF + i * P
+            res = keep.tile([P, 2, P], F32, name=f"end{i}")
+            nc.vector.tensor_tensor(res[:], pair[:], last[:, :, i * P : (i + 1) * P], ALU.add)
+            nc.sync.dma_start(out[:, a : a + P].rearrange("(b p) v -> p b v", p=P), res[:])
+
+        centre = psum.tile([P, 2, N], F32, name="centre", tag="bank0")
+        neighbour = psum.tile([P, 2, N], F32, name="neighbour", tag="bank1")
+        last = keep.tile([P, 2, HALF], F32, name="last")
+        product(1, 0, 256, 4, True)
+        product(1, 256, 512, 5, True)
+        plain_c0 = plain(0, cen_t, "c")
+        plain_n0 = plain(0, pos1_t, "n")
+        product(1, 512, 1024, 7)
+        turn_in(centre, 0, plain_c0)
+        turn_in(neighbour, 0, plain_n0)
+        there0 = add_up(0, three_terms(0), 2)
         turn_in(centre, 1, plain(1, cen_t, "c"))
         turn_in(neighbour, 1, plain(1, pos1_t, "n"))
+        parts1 = three_terms(1)
         back0 = turn_back(0, there0)
-        there1 = summed_band(1)
-        pairs = [pair_up(0, [scale(centre, 0, 0), scale(neighbour, 1, 0)])]
-        last = keep.tile([P, 2, HALF], F32, name="last")
+        pairs = [psum.tile([P, 2, P], F32, name=f"pair{i}", tag=f"bank{5 + i}") for i in range(2)]
+        scale_back(pairs[0], centre, 0, 0)
+        scale_back(pairs[1], centre, 0, 1)
+        there1 = add_up(1, parts1, 3)
+        scale_back(pairs[0], neighbour, 1, 0)
+        scale_back(pairs[1], neighbour, 1, 1)
         for b in range(2):
-            fused(last[:, b, :], b, pos2_t, second[:, HALF:], HALF, V)
-        scaled_c = scale(centre, 0, 1)
+            fused(last[:, b, :], b, pos2_t, second[:], HALF, V)
         back1 = turn_back(1, there1)
-        pairs.append(pair_up(1, [scaled_c, scale(neighbour, 1, 1)]))
-        leave(0, back0)
-        leave(1, back1)
+        finish_first(0, back0)
+        finish_first(1, back1)
         for i in range(2):
-            res = keep.tile([P, 2, P], F32, name=f"end{i}")
-            nc.vector.tensor_tensor(res[:], pairs[i][:], last[:, :, i * P : (i + 1) * P], ALU.add)
-            a = HALF + i * P
-            nc.sync.dma_start(out[:, a : a + P].rearrange("(b p) v -> p b v", p=P), res[:])
+            finish_second(i, pairs[i])

@@ -82,7 +82,7 @@ def tile_picked_grand_relu_p_kernel(tc, x_words, x_scales, w1, gate, offs, cen, 
                 grouped[:].rearrange("p (c i) j -> p c j i", i=PACK),
                 w_raw[:, :, b * P : (b + 1) * P].rearrange("p j (c i) -> p c j i", i=PACK),
             )
-            w_codes.append(keep.tile([P, P], U32, name=f"w_codes{b}", align_bytes=64))
+            w_codes.append(keep.tile([P, P], U32, name=f"w_codes{b}", tag=f"w_codes{b}", align_bytes=64))
             w_scale.append(keep.tile([P, P], U8, name=f"w_scale{b}", align_bytes=64))
             nc.vector.quantize_mx(
                 out=w_codes[b][:].bitcast(FP8X4), scales=w_scale[b][:], in_=grouped[:].rearrange("p m j -> p (m j)")
@@ -126,8 +126,8 @@ def tile_picked_grand_relu_p_kernel(tc, x_words, x_scales, w1, gate, offs, cen, 
         def fused(part, b, lst, factor, v0, v1):
             nc.vector.tensor_tensor(part, y[b][:].indirect(lst[:, v0 // LANES : v1 // LANES]), factor, ALU.mult)
 
-        def plain(b, lst, name):
-            part = keep.tile([P, HALF], F32, name=f"plain{name}{b}")
+        def plain(b, lst, name, tag=None):
+            part = keep.tile([P, HALF], F32, name=f"plain{name}{b}", tag=tag or f"plain{name}{b}", align_bytes=64)
             nc.scalar.activation(part[:], y[b][:].indirect(lst[:, HALF // LANES :]), ACT.Copy)
             return part
 
@@ -160,50 +160,50 @@ def tile_picked_grand_relu_p_kernel(tc, x_words, x_scales, w1, gate, offs, cen, 
             for i in range(2):
                 nc.tensor.transpose(there[:, i, b * P : (b + 1) * P], part[:, i * P : (i + 1) * P], ident[:])
 
-        def scale_back(pair, there, d, i):
-            scaled = keep.tile([P, N], F32, name=f"scaled{d}_{i}")
-            nc.scalar.activation(
-                scaled[:], there[:, i, :], ACT.Copy, scale=(own_cols[:], cols[:, 0, :])[d][:, i : i + 1]
+        def scale_centre(i):
+            scaled = keep.tile([P, N], F32, name=f"scaled{i}", tag=f"scaled{i}")
+            nc.scalar.activation(scaled[:], centre[:, i, :], ACT.Copy, scale=own_cols[:, i : i + 1])
+            return scaled
+
+        def join_back(i, scaled):
+            joined = keep.tile([P, N], F32, name=f"joined{i}")
+            nc.vector.scalar_tensor_tensor(
+                joined[:], neighbour[:, i, :], cols[:, 0, i : i + 1], scaled[:], ALU.mult, ALU.add
             )
             for b in range(2):
-                turn(pair[:, b, :], scaled[:, b * P : (b + 1) * P], (d, b) == (0, 0), (d, b) == (1, 1))
+                nc.tensor.transpose(pairs[b][:, i * P : (i + 1) * P], joined[:, b * P : (b + 1) * P], ident[:])
 
         def finish_first(b, back):
             res = keep.tile([P, HALF], F32, name=f"res{b}")
             nc.scalar.copy(res[:], back[:])
             (nc.sync, nc.scalar)[b].dma_start(out[b * P : (b + 1) * P, :HALF], res[:])
 
-        def finish_second(i, pair):
-            a = HALF + i * P
-            res = keep.tile([P, 2, P], F32, name=f"end{i}")
-            nc.vector.tensor_tensor(res[:], pair[:], last[:, :, i * P : (i + 1) * P], ALU.add)
-            nc.sync.dma_start(out[:, a : a + P].rearrange("(b p) v -> p b v", p=P), res[:])
+        def finish_second(b):
+            res = keep.tile([P, HALF], F32, name=f"end{b}")
+            nc.vector.tensor_tensor(res[:], pairs[b][:], last[b][:], ALU.add)
+            nc.sync.dma_start(out[b * P : (b + 1) * P, HALF:], res[:])
 
         centre = psum.tile([P, 2, N], F32, name="centre", tag="bank0")
         neighbour = psum.tile([P, 2, N], F32, name="neighbour", tag="bank1")
-        last = keep.tile([P, 2, HALF], F32, name="last")
-        product(1, 0, 256, 4, True)
-        product(1, 256, 512, 5, True)
+        pairs = [psum.tile([P, HALF], F32, name=f"pair{b}", tag=f"bank{5 + b}") for b in range(2)]
         plain_c0 = plain(0, cen_t, "c")
-        plain_n0 = plain(0, pos1_t, "n")
+        product(1, 0, 512, 4)
         product(1, 512, 1024, 7)
         turn_in(centre, 0, plain_c0)
-        turn_in(neighbour, 0, plain_n0)
         there0 = add_up(0, three_terms(0), 2)
         turn_in(centre, 1, plain(1, cen_t, "c"))
+        turn_in(neighbour, 0, plain(0, pos1_t, "n", "w_codes1"))
         turn_in(neighbour, 1, plain(1, pos1_t, "n"))
-        parts1 = three_terms(1)
-        back0 = turn_back(0, there0)
-        pairs = [psum.tile([P, 2, P], F32, name=f"pair{i}", tag=f"bank{5 + i}") for i in range(2)]
-        scale_back(pairs[0], centre, 0, 0)
-        scale_back(pairs[1], centre, 0, 1)
-        there1 = add_up(1, parts1, 3)
-        scale_back(pairs[0], neighbour, 1, 0)
-        scale_back(pairs[1], neighbour, 1, 1)
-        for b in range(2):
-            fused(last[:, b, :], b, pos2_t, second[:], HALF, V)
-        back1 = turn_back(1, there1)
-        finish_first(0, back0)
-        finish_first(1, back1)
+        there1 = add_up(1, three_terms(1), 3)
+        scaled = [scale_centre(i) for i in range(2)]
+        last = [keep.tile([P, HALF], F32, name="last0")]
+        fused(last[0][:], 0, pos2_t, second[:], HALF, V)
         for i in range(2):
-            finish_second(i, pairs[i])
+            join_back(i, scaled[i])
+        last.append(keep.tile([P, HALF], F32, name="last1", tag="scaled0"))
+        fused(last[1][:], 1, pos2_t, second[:], HALF, V)
+        backs = [turn_back(0, there0), turn_back(1, there1)]
+        for b in range(2):
+            finish_first(b, backs[b])
+        for b in range(2):
+            finish_second(b)

@@ -126,9 +126,9 @@ def tile_picked_grand_relu_p_kernel(tc, x_words, x_scales, w1, gate, offs, cen, 
         def fused(part, b, lst, factor, v0, v1):
             nc.vector.tensor_tensor(part, y[b][:].indirect(lst[:, v0 // LANES : v1 // LANES]), factor, ALU.mult)
 
-        def plain(b, lst, name, tag=None):
+        def plain(b, lst, name, tag=None, v0=HALF):
             part = keep.tile([P, HALF], F32, name=f"plain{name}{b}", tag=tag or f"plain{name}{b}", align_bytes=64)
-            nc.scalar.activation(part[:], y[b][:].indirect(lst[:, HALF // LANES :]), ACT.Copy)
+            nc.scalar.activation(part[:], y[b][:].indirect(lst[:, v0 // LANES : (v0 + HALF) // LANES]), ACT.Copy)
             return part
 
         def turn(acc, part, start, stop):
@@ -176,7 +176,7 @@ def tile_picked_grand_relu_p_kernel(tc, x_words, x_scales, w1, gate, offs, cen, 
         def finish_first(b, back):
             res = keep.tile([P, HALF], F32, name=f"res{b}")
             nc.scalar.copy(res[:], back[:])
-            (nc.sync, nc.scalar)[b].dma_start(out[b * P : (b + 1) * P, :HALF], res[:])
+            nc.scalar.dma_start(out[b * P : (b + 1) * P, :HALF], res[:])
 
         def finish_second(b):
             res = keep.tile([P, HALF], F32, name=f"end{b}")
@@ -186,24 +186,32 @@ def tile_picked_grand_relu_p_kernel(tc, x_words, x_scales, w1, gate, offs, cen, 
         centre = psum.tile([P, 2, N], F32, name="centre", tag="bank0")
         neighbour = psum.tile([P, 2, N], F32, name="neighbour", tag="bank1")
         pairs = [psum.tile([P, HALF], F32, name=f"pair{b}", tag=f"bank{5 + b}") for b in range(2)]
+        last = [keep.tile([P, HALF], F32, name=f"last{b}") for b in range(2)]
         plain_c0 = plain(0, cen_t, "c")
         product(1, 0, 512, 4)
         product(1, 512, 1024, 7)
         turn_in(centre, 0, plain_c0)
         there0 = add_up(0, three_terms(0), 2)
+        fused(last[0][:], 0, pos2_t, second[:], HALF, V)
         turn_in(centre, 1, plain(1, cen_t, "c"))
         turn_in(neighbour, 0, plain(0, pos1_t, "n", "w_codes1"))
         turn_in(neighbour, 1, plain(1, pos1_t, "n"))
-        there1 = add_up(1, three_terms(1), 3)
+        near = [keep.tile([P, HALF], F32, name=f"near{d}") for d in range(2)]
+        for d, lst in enumerate((pos1_t, pos2_t)):
+            fused(near[d][:], 1, lst, first[:, d, :], 0, HALF)
+        fused(last[1][:], 1, pos2_t, second[:], HALF, V)
+        back0 = turn_back(0, there0)
         scaled = [scale_centre(i) for i in range(2)]
-        last = [keep.tile([P, HALF], F32, name="last0")]
-        fused(last[0][:], 0, pos2_t, second[:], HALF, V)
+        here = plain(1, cen_t, "h", "plainn1", 0)
+        finish_first(0, back0)
         for i in range(2):
             join_back(i, scaled[i])
-        last.append(keep.tile([P, HALF], F32, name="last1", tag="scaled0"))
-        fused(last[1][:], 1, pos2_t, second[:], HALF, V)
-        backs = [turn_back(0, there0), turn_back(1, there1)]
-        for b in range(2):
-            finish_first(b, backs[b])
-        for b in range(2):
-            finish_second(b)
+        both = keep.tile([P, HALF], F32, name="both", tag="scaled0")
+        nc.vector.tensor_tensor(both[:], near[0][:], near[1][:], ALU.add)
+        stay = keep.tile([P, HALF], F32, name="stay")
+        nc.vector.tensor_tensor(stay[:], here[:], own[:], ALU.mult)
+        finish_second(0)
+        res = keep.tile([P, HALF], F32, name="res1")
+        nc.vector.tensor_tensor(res[:], stay[:], both[:], ALU.add)
+        nc.sync.dma_start(out[P:, :HALF], res[:])
+        finish_second(1)

@@ -64,8 +64,8 @@ def tile_picked_grand_relu_p_kernel(tc, x_words, x_scales, w1, gate, offs, cen, 
         x_codes = [keep.tile([P, CUT], U32, name="x_codes0", align_bytes=64)]
         nc.vector.tensor_copy(x_codes[0][:], word_tab[:].bitcast(U32).indirect(offs_t[:, : CUT // LANES]))
 
-        second = turns.tile([P, HALF], F32, name="second", offset=0)
-        nc.sync.dma_start(second[:], gate[1, :, HALF:])
+        second = turns.tile([P, V], F32, name="second", offset=0)
+        nc.sync.dma_start(second[:], gate[1])
         cols = keep.tile([P, 2, 8], F32, name="cols", tag="picked", align_bytes=64)
         with nc.allow_non_contiguous_dma(reason="one gate value a partition"):
             for d in range(2):
@@ -93,8 +93,8 @@ def tile_picked_grand_relu_p_kernel(tc, x_words, x_scales, w1, gate, offs, cen, 
 
         less = keep.tile([P, HALF], F32, name="less")
         nc.scalar.activation(less[:], first[:, 0, :], ACT.Identity, bias=1.0, scale=-1.0)
-        own = keep.tile([P, HALF], F32, name="own")
-        nc.vector.tensor_tensor(own[:], less[:], first[:, 1, :], ALU.subtract)
+        own = turns.tile([P, HALF], F32, name="own", offset=T + BAND_BYTES)
+        nc.gpsimd.tensor_tensor(own[:], less[:], first[:, 1, :], ALU.subtract)
 
         y = [keep.tile([P, S], F32, name=f"y{b}") for b in range(2)]
 
@@ -119,7 +119,7 @@ def tile_picked_grand_relu_p_kernel(tc, x_words, x_scales, w1, gate, offs, cen, 
             )
 
         for i in range(3):
-            product(0, i * 256, (i + 1) * 256, i, i % 2 == 0)
+            product(0, i * 256, (i + 1) * 256, i, i == 2)
         product(0, 768, 896, 3)
         product(0, 896, 1024, 7, True)
 
@@ -134,12 +134,10 @@ def tile_picked_grand_relu_p_kernel(tc, x_words, x_scales, w1, gate, offs, cen, 
         def turn(acc, part, start, stop):
             nc.tensor.matmul(acc, part, ident[:], start=start, stop=stop, is_transpose=True)
 
-        def three_terms(b):
-            parts = []
-            for t, (lst, factor) in enumerate(((pos1_t, first[:, 0, :]), (pos2_t, first[:, 1, :]), (cen_t, own[:]))):
-                parts.append(keep.tile([P, HALF], F32, name=f"part{b}_{t}"))
-                fused(parts[t][:], b, lst, factor, 0, HALF)
-            return parts
+        def term(b, lst, factor, width, name):
+            part = keep.tile([P, width], F32, name=f"{name}{b}")
+            fused(part[:], b, lst, factor, 0, width)
+            return part
 
         def add_up(b, parts, bank):
             there = psum.tile([P, 2, P], F32, name=f"there{b}", tag=f"bank{bank}")
@@ -180,38 +178,36 @@ def tile_picked_grand_relu_p_kernel(tc, x_words, x_scales, w1, gate, offs, cen, 
 
         def finish_second(b):
             res = keep.tile([P, HALF], F32, name=f"end{b}")
-            nc.vector.tensor_tensor(res[:], pairs[b][:], last[b][:], ALU.add)
+            nc.vector.tensor_tensor(res[:], pairs[b][:], last[b][:, HALF:], ALU.add)
             nc.sync.dma_start(out[b * P : (b + 1) * P, HALF:], res[:])
 
         centre = psum.tile([P, 2, N], F32, name="centre", tag="bank0")
         neighbour = psum.tile([P, 2, N], F32, name="neighbour", tag="bank1")
         pairs = [psum.tile([P, HALF], F32, name=f"pair{b}", tag=f"bank{5 + b}") for b in range(2)]
-        last = [keep.tile([P, HALF], F32, name=f"last{b}") for b in range(2)]
         plain_c0 = plain(0, cen_t, "c")
         product(1, 0, 512, 4)
         product(1, 512, 1024, 7)
         turn_in(centre, 0, plain_c0)
-        there0 = add_up(0, three_terms(0), 2)
-        fused(last[0][:], 0, pos2_t, second[:], HALF, V)
+        near = [term(0, pos1_t, first[:, 0, :], HALF, "near")]
+        last = [term(0, pos2_t, second[:], V, "last")]
+        there0 = add_up(0, [near[0], last[0], term(0, cen_t, own[:], HALF, "self")], 2)
         turn_in(centre, 1, plain(1, cen_t, "c"))
         turn_in(neighbour, 0, plain(0, pos1_t, "n", "w_codes1"))
         turn_in(neighbour, 1, plain(1, pos1_t, "n"))
-        near = [keep.tile([P, HALF], F32, name=f"near{d}") for d in range(2)]
-        for d, lst in enumerate((pos1_t, pos2_t)):
-            fused(near[d][:], 1, lst, first[:, d, :], 0, HALF)
-        fused(last[1][:], 1, pos2_t, second[:], HALF, V)
+        near.append(term(1, pos1_t, first[:, 0, :], HALF, "near"))
+        last.append(term(1, pos2_t, second[:], V, "last"))
         back0 = turn_back(0, there0)
         scaled = [scale_centre(i) for i in range(2)]
         here = plain(1, cen_t, "h", "plainn1", 0)
         finish_first(0, back0)
         for i in range(2):
             join_back(i, scaled[i])
-        both = keep.tile([P, HALF], F32, name="both", tag="scaled0")
-        nc.vector.tensor_tensor(both[:], near[0][:], near[1][:], ALU.add)
+        both = keep.tile([P, HALF], F32, name="both")
+        nc.gpsimd.tensor_tensor(both[:], near[1][:], last[1][:, :HALF], ALU.add)
         stay = keep.tile([P, HALF], F32, name="stay")
         nc.vector.tensor_tensor(stay[:], here[:], own[:], ALU.mult)
-        finish_second(0)
         res = keep.tile([P, HALF], F32, name="res1")
-        nc.vector.tensor_tensor(res[:], stay[:], both[:], ALU.add)
-        nc.sync.dma_start(out[P:, :HALF], res[:])
-        finish_second(1)
+        nc.gpsimd.tensor_tensor(res[:], stay[:], both[:], ALU.add)
+        nc.scalar.dma_start(out[P:, :HALF], res[:])
+        for b in range(2):
+            finish_second(b)

@@ -38,25 +38,26 @@ def tile_picked_grand_relu_p_kernel(tc, x_words, x_scales, w1, gate, offs, cen, 
         cen_t = keep.tile([P, V // LANES], U16, name="cen_t")
         pos1_t = keep.tile([P, V // LANES], U16, name="pos1_t")
         pos2_t = keep.tile([P, V // LANES], U16, name="pos2_t")
-        scale_tab = turns.tile([P, T], U8, name="scale_tab", offset=0, align_bytes=64)
+        scale_tab = keep.tile([P, T], U8, name="scale_tab", align_bytes=64)
         word_tab = keep.tile([P, T], I32, name="word_tab", align_bytes=64)
         w_raw = keep.tile([P, PACK, N], F32, name="w_raw")
-        first = keep.tile([P, 2, HALF], F32, name="first")
+        gate_rows = keep.tile([P, P], F32, name="gate_rows")
 
         nc.vector.memset(scale_tab[:FIRST, :].bitcast(I32), 0)
         nc.scalar.dma_start(scale_tab[FIRST:, :].bitcast(I32), x_scales[0].bitcast(I32))
         nc.sync.dma_start(offs_t[:], offs)
+        middle = gate.rearrange("d p v -> (d p) v")[P - LANES : P + LANES, :]
+        nc.sync.dma_start(gate_rows[:], middle.rearrange("r (b c) -> (r b) c", c=P))
         nc.sync.dma_start(word_tab[:], x_words[0].rearrange("p n t -> p (n t)").bitcast(I32))
+        nc.sync.dma_start(w_raw[:], w1.rearrange("(p j) m -> p j m", j=PACK))
         nc.sync.dma_start(cen_t[:], cen)
         nc.sync.dma_start(pos1_t[:], pos1)
         nc.sync.dma_start(pos2_t[:], pos2)
-        nc.sync.dma_start(w_raw[:], w1.rearrange("(p j) m -> p j m", j=PACK))
-        nc.sync.dma_start(first[:], gate[:, :, :HALF].rearrange("d p v -> p d v"))
 
         ident = keep.tile([P, P], F32, name="ident")
         make_identity(nc, ident[:])
 
-        picked = keep.tile([P, S], U8, name="picked", tag="picked", align_bytes=64)
+        picked = keep.tile([P, S], U8, name="picked", align_bytes=64)
         nc.vector.tensor_copy(picked[:], scale_tab[:].indirect(offs_t[:]))
         x_scale = keep.tile([P, S], U8, name="x_scale", align_bytes=64)
         for r in range(PACK):
@@ -64,20 +65,32 @@ def tile_picked_grand_relu_p_kernel(tc, x_words, x_scales, w1, gate, offs, cen, 
         x_codes = [keep.tile([P, CUT], U32, name="x_codes0", align_bytes=64)]
         nc.vector.tensor_copy(x_codes[0][:], word_tab[:].bitcast(U32).indirect(offs_t[:, : CUT // LANES]))
 
-        second = turns.tile([P, V], F32, name="second", offset=0)
-        nc.sync.dma_start(second[:], gate[1])
-        cols = keep.tile([P, 2, 8], F32, name="cols", tag="picked", align_bytes=64)
-        with nc.allow_non_contiguous_dma(reason="one gate value a partition"):
-            for d in range(2):
-                nc.sync.dma_start(cols[:, d, :2], gate[d, 0, HALF:].rearrange("(i p) -> p i", p=P))
-        rest = keep.tile([P, 2], F32, name="rest")
-        own_cols = keep.tile([P, 2], F32, name="own_cols")
-        nc.gpsimd.tensor_scalar(rest[:], cols[:, 0, :2], -1.0, 1.0, ALU.mult, ALU.add)
-        nc.gpsimd.tensor_tensor(own_cols[:], rest[:], cols[:, 1, :2], ALU.subtract)
+        turned = psum.tile([P, P], F32, name="turned", tag="bank7")
+        nc.tensor.transpose(turned[:], gate_rows[:], ident[:])
+        cols = turns.tile([P, 3, BLOCKS], F32, name="cols", offset=BAND_BYTES - 32)
+        late = keep.tile([P, 2, 2], F32, name="late")
+        nc.scalar.copy(cols[:, :2, :], turned[:].rearrange("p (d q) -> p d q", d=2)[:, :, :BLOCKS])
+        rest = keep.tile([P, BLOCKS], F32, name="rest")
+        nc.scalar.activation(rest[:], turned[:, :BLOCKS], ACT.Identity, bias=1.0, scale=-1.0)
+        for j in range(BLOCKS):
+            own = cols[:, 2, j : j + 1] if j < 2 else late[:, 0, j - 2 : j - 1]
+            nc.scalar.activation(own, cols[:, 1, j : j + 1], ACT.Identity, bias=rest[:, j : j + 1], scale=-1.0)
+        nc.scalar.copy(late[:, 1, :], cols[:, 0, 2:])
+
+        def spread(name, picks, bank):
+            wide = psum.tile([P, len(picks) * P], F32, name=f"wide_{name}", tag=f"bank{bank}")
+            for i, (d, j) in enumerate(picks):
+                nc.tensor.transpose(wide[:, i * P : (i + 1) * P], cols[:, d, j : j + 1].to_broadcast([P, P]), ident[:])
+            factor = keep.tile([P, len(picks) * P], F32, name=f"factor_{name}")
+            nc.scalar.copy(factor[:], wide[:])
+            return factor
+
+        first = spread("first", [(0, 0), (0, 1), (2, 0), (2, 1)], 5)
+        second = spread("second", [(1, j) for j in range(BLOCKS)], 6)
 
         w_codes, w_scale = [], []
         for b in range(2):
-            grouped = turns.tile([P, P, PACK], BF16, name=f"grouped{b}", offset=T + b * BAND_BYTES, align_bytes=64)
+            grouped = turns.tile([P, P, PACK], BF16, name=f"grouped{b}", offset=b * BAND_BYTES, align_bytes=64)
             nc.scalar.copy(
                 grouped[:].rearrange("p (c i) j -> p c j i", i=PACK),
                 w_raw[:, :, b * P : (b + 1) * P].rearrange("p j (c i) -> p c j i", i=PACK),
@@ -88,14 +101,10 @@ def tile_picked_grand_relu_p_kernel(tc, x_words, x_scales, w1, gate, offs, cen, 
                 out=w_codes[b][:].bitcast(FP8X4), scales=w_scale[b][:], in_=grouped[:].rearrange("p m j -> p (m j)")
             )
             if b == 0:
-                x_codes.append(turns.tile([P, S - CUT], U32, name="x_codes1", offset=T, align_bytes=64))
+                x_codes.append(turns.tile([P, S - CUT], U32, name="x_codes1", offset=0, align_bytes=64))
                 nc.vector.tensor_copy(x_codes[1][:], word_tab[:].bitcast(U32).indirect(offs_t[:, CUT // LANES :]))
 
-        less = keep.tile([P, HALF], F32, name="less")
-        nc.scalar.activation(less[:], first[:, 0, :], ACT.Identity, bias=1.0, scale=-1.0)
-        own = turns.tile([P, HALF], F32, name="own", offset=T + BAND_BYTES)
-        nc.gpsimd.tensor_tensor(own[:], less[:], first[:, 1, :], ALU.subtract)
-
+        own = first[:, HALF:]
         y = [keep.tile([P, S], F32, name=f"y{b}") for b in range(2)]
 
         def product(b, a0, z0, bank, on_vector=False):
@@ -160,13 +169,13 @@ def tile_picked_grand_relu_p_kernel(tc, x_words, x_scales, w1, gate, offs, cen, 
 
         def scale_centre(i):
             scaled = keep.tile([P, N], F32, name=f"scaled{i}", tag=f"scaled{i}")
-            nc.scalar.activation(scaled[:], centre[:, i, :], ACT.Copy, scale=own_cols[:, i : i + 1])
+            nc.scalar.activation(scaled[:], centre[:, i, :], ACT.Copy, scale=late[:, 0, i : i + 1])
             return scaled
 
         def join_back(i, scaled):
             joined = keep.tile([P, N], F32, name=f"joined{i}")
             nc.vector.scalar_tensor_tensor(
-                joined[:], neighbour[:, i, :], cols[:, 0, i : i + 1], scaled[:], ALU.mult, ALU.add
+                joined[:], neighbour[:, i, :], late[:, 1, i : i + 1], scaled[:], ALU.mult, ALU.add
             )
             for b in range(2):
                 nc.tensor.transpose(pairs[b][:, i * P : (i + 1) * P], joined[:, b * P : (b + 1) * P], ident[:])
@@ -188,13 +197,13 @@ def tile_picked_grand_relu_p_kernel(tc, x_words, x_scales, w1, gate, offs, cen, 
         product(1, 0, 512, 4)
         product(1, 512, 1024, 7)
         turn_in(centre, 0, plain_c0)
-        near = [term(0, pos1_t, first[:, 0, :], HALF, "near")]
+        near = [term(0, pos1_t, first[:, :HALF], HALF, "near")]
         last = [term(0, pos2_t, second[:], V, "last")]
-        there0 = add_up(0, [near[0], last[0], term(0, cen_t, own[:], HALF, "self")], 2)
+        there0 = add_up(0, [near[0], last[0], term(0, cen_t, own, HALF, "self")], 2)
         turn_in(centre, 1, plain(1, cen_t, "c"))
         turn_in(neighbour, 0, plain(0, pos1_t, "n", "w_codes1"))
         turn_in(neighbour, 1, plain(1, pos1_t, "n"))
-        near.append(term(1, pos1_t, first[:, 0, :], HALF, "near"))
+        near.append(term(1, pos1_t, first[:, :HALF], HALF, "near"))
         last.append(term(1, pos2_t, second[:], V, "last"))
         back0 = turn_back(0, there0)
         scaled = [scale_centre(i) for i in range(2)]
@@ -202,12 +211,12 @@ def tile_picked_grand_relu_p_kernel(tc, x_words, x_scales, w1, gate, offs, cen, 
         finish_first(0, back0)
         for i in range(2):
             join_back(i, scaled[i])
-        both = keep.tile([P, HALF], F32, name="both")
-        nc.gpsimd.tensor_tensor(both[:], near[1][:], last[1][:, :HALF], ALU.add)
+        both = keep.tile([P, HALF], F32, name="both", tag="scaled0")
+        nc.vector.tensor_tensor(both[:], near[1][:], last[1][:, :HALF], ALU.add)
         stay = keep.tile([P, HALF], F32, name="stay")
-        nc.vector.tensor_tensor(stay[:], here[:], own[:], ALU.mult)
+        nc.vector.tensor_tensor(stay[:], here[:], own, ALU.mult)
+        finish_second(0)
         res = keep.tile([P, HALF], F32, name="res1")
-        nc.gpsimd.tensor_tensor(res[:], stay[:], both[:], ALU.add)
-        nc.scalar.dma_start(out[P:, :HALF], res[:])
-        for b in range(2):
-            finish_second(b)
+        nc.vector.tensor_tensor(res[:], stay[:], both[:], ALU.add)
+        nc.sync.dma_start(out[P:, :HALF], res[:])
+        finish_second(1)

@@ -40,7 +40,7 @@ def tile_picked_grand_relu_p_kernel(tc, x_words, x_scales, w1, gate, offs, cen, 
         pos2_t = keep.tile([P, V // LANES], U16, name="pos2_t")
         scale_tab = keep.tile([P, T], U8, name="scale_tab", align_bytes=64)
         word_tab = keep.tile([P, T], I32, name="word_tab", align_bytes=64)
-        w_raw = keep.tile([P, PACK, N], F32, name="w_raw")
+        w_raw = keep.tile([P, PACK, N], F32, name="w_raw", tag="w_raw")
         gate_rows = keep.tile([P, P], F32, name="gate_rows")
 
         nc.vector.memset(scale_tab[:FIRST, :].bitcast(I32), 0)
@@ -67,26 +67,32 @@ def tile_picked_grand_relu_p_kernel(tc, x_words, x_scales, w1, gate, offs, cen, 
 
         turned = psum.tile([P, P], F32, name="turned", tag="bank7")
         nc.tensor.transpose(turned[:], gate_rows[:], ident[:])
-        cols = turns.tile([P, 3, BLOCKS], F32, name="cols", offset=BAND_BYTES - 32)
-        late = keep.tile([P, 2, 2], F32, name="late")
-        nc.scalar.copy(cols[:, :2, :], turned[:].rearrange("p (d q) -> p d q", d=2)[:, :, :BLOCKS])
+        cols1 = turns.tile([P, 2, 8], F32, name="cols1", offset=BAND_BYTES - 32)
+        cols0 = keep.tile([P, BLOCKS], F32, name="cols0")
         rest = keep.tile([P, BLOCKS], F32, name="rest")
+        own_early = keep.tile([P, 2], F32, name="own_early")
+        own_late = [
+            turns.tile([P, 1], F32, name="own_late0", offset=2 * BAND_BYTES + P * 4),
+            keep.tile([P, 1], F32, name="own_late1"),
+        ]
+        nc.scalar.copy(cols1[:, :, :2], turned[:, P // 2 : P // 2 + BLOCKS].rearrange("p (a b) -> p a b", a=2))
+        nc.scalar.copy(cols0[:], turned[:, :BLOCKS])
         nc.scalar.activation(rest[:], turned[:, :BLOCKS], ACT.Identity, bias=1.0, scale=-1.0)
         for j in range(BLOCKS):
-            own = cols[:, 2, j : j + 1] if j < 2 else late[:, 0, j - 2 : j - 1]
-            nc.scalar.activation(own, cols[:, 1, j : j + 1], ACT.Identity, bias=rest[:, j : j + 1], scale=-1.0)
-        nc.scalar.copy(late[:, 1, :], cols[:, 0, 2:])
+            own = own_early[:, j : j + 1] if j < 2 else own_late[j - 2][:]
+            nc.scalar.activation(
+                own, turned[:, P // 2 + j : P // 2 + j + 1], ACT.Identity, bias=rest[:, j : j + 1], scale=-1.0
+            )
 
-        def spread(name, picks, bank):
-            wide = psum.tile([P, len(picks) * P], F32, name=f"wide_{name}", tag=f"bank{bank}")
-            for i, (d, j) in enumerate(picks):
-                nc.tensor.transpose(wide[:, i * P : (i + 1) * P], cols[:, d, j : j + 1].to_broadcast([P, P]), ident[:])
-            factor = keep.tile([P, len(picks) * P], F32, name=f"factor_{name}")
-            nc.scalar.copy(factor[:], wide[:])
-            return factor
+        def spread(columns, bank):
+            wide = psum.tile([P, V], F32, name=f"wide{bank}", tag=f"bank{bank}")
+            for i, column in enumerate(columns):
+                nc.tensor.transpose(wide[:, i * P : (i + 1) * P], column.to_broadcast([P, P]), ident[:])
+            return wide
 
-        first = spread("first", [(0, 0), (0, 1), (2, 0), (2, 1)], 5)
-        second = spread("second", [(1, j) for j in range(BLOCKS)], 6)
+        second = keep.tile([P, V], F32, name="second")
+        nc.scalar.copy(second[:], spread([cols1[:, j // 2, j % 2 : j % 2 + 1] for j in range(BLOCKS)], 6)[:])
+        wide_first = spread([t[:, j : j + 1] for t in (cols0, own_early) for j in range(2)], 5)
 
         w_codes, w_scale = [], []
         for b in range(2):
@@ -104,6 +110,8 @@ def tile_picked_grand_relu_p_kernel(tc, x_words, x_scales, w1, gate, offs, cen, 
                 x_codes.append(turns.tile([P, S - CUT], U32, name="x_codes1", offset=0, align_bytes=64))
                 nc.vector.tensor_copy(x_codes[1][:], word_tab[:].bitcast(U32).indirect(offs_t[:, CUT // LANES :]))
 
+        first = keep.tile([P, V], F32, name="first", tag="w_raw")
+        nc.scalar.copy(first[:], wide_first[:])
         own = first[:, HALF:]
         y = [keep.tile([P, S], F32, name=f"y{b}") for b in range(2)]
 
@@ -135,17 +143,24 @@ def tile_picked_grand_relu_p_kernel(tc, x_words, x_scales, w1, gate, offs, cen, 
         def fused(part, b, lst, factor, v0, v1):
             nc.vector.tensor_tensor(part, y[b][:].indirect(lst[:, v0 // LANES : v1 // LANES]), factor, ALU.mult)
 
-        def plain(b, lst, name, tag=None, v0=HALF):
-            part = keep.tile([P, HALF], F32, name=f"plain{name}{b}", tag=tag or f"plain{name}{b}", align_bytes=64)
-            nc.scalar.activation(part[:], y[b][:].indirect(lst[:, v0 // LANES : (v0 + HALF) // LANES]), ACT.Copy)
+        def plain(part, b, lst, v0, v1):
+            nc.scalar.activation(part, y[b][:].indirect(lst[:, v0 // LANES : v1 // LANES]), ACT.Copy)
+
+        def centre_in(b):
+            part = keep.tile([P, HALF], F32, name=f"plain_centre{b}")
+            plain(part[:], b, cen_t, HALF, V)
             return part
+
+        def neighbour_in(part, b, i):
+            plain(part, b, pos1_t, HALF + i * P, HALF + (i + 1) * P)
+            nc.tensor.transpose(neighbours[i][:, b * P : (b + 1) * P], part, ident[:])
 
         def turn(acc, part, start, stop):
             nc.tensor.matmul(acc, part, ident[:], start=start, stop=stop, is_transpose=True)
 
-        def term(b, lst, factor, width, name):
-            part = keep.tile([P, width], F32, name=f"{name}{b}")
-            fused(part[:], b, lst, factor, 0, width)
+        def term(b, lst, factor, name):
+            part = keep.tile([P, HALF], F32, name=f"{name}{b}")
+            fused(part[:], b, lst, factor, 0, HALF)
             return part
 
         def add_up(b, parts, bank):
@@ -169,50 +184,58 @@ def tile_picked_grand_relu_p_kernel(tc, x_words, x_scales, w1, gate, offs, cen, 
 
         def scale_centre(i):
             scaled = keep.tile([P, N], F32, name=f"scaled{i}", tag=f"scaled{i}")
-            nc.scalar.activation(scaled[:], centre[:, i, :], ACT.Copy, scale=late[:, 0, i : i + 1])
+            nc.scalar.activation(scaled[:], centre[:, i, :], ACT.Copy, scale=own_late[i][:])
             return scaled
 
         def join_back(i, scaled):
             joined = keep.tile([P, N], F32, name=f"joined{i}")
             nc.vector.scalar_tensor_tensor(
-                joined[:], neighbour[:, i, :], late[:, 1, i : i + 1], scaled[:], ALU.mult, ALU.add
+                joined[:], neighbours[i][:], cols0[:, 2 + i : 3 + i], scaled[:], ALU.mult, ALU.add
             )
             for b in range(2):
-                nc.tensor.transpose(pairs[b][:, i * P : (i + 1) * P], joined[:, b * P : (b + 1) * P], ident[:])
+                nc.tensor.transpose(pairs[i][:, b, :], joined[:, b * P : (b + 1) * P], ident[:])
 
         def finish_first(b, back):
             res = keep.tile([P, HALF], F32, name=f"res{b}")
             nc.scalar.copy(res[:], back[:])
             nc.scalar.dma_start(out[b * P : (b + 1) * P, :HALF], res[:])
 
-        def finish_second(b):
-            res = keep.tile([P, HALF], F32, name=f"end{b}")
-            nc.vector.tensor_tensor(res[:], pairs[b][:], last[b][:, HALF:], ALU.add)
-            nc.sync.dma_start(out[b * P : (b + 1) * P, HALF:], res[:])
+        def finish_second(i):
+            a = HALF + i * P
+            res = keep.tile([P, 2, P], F32, name=f"end{i}")
+            nc.vector.tensor_tensor(res[:], pairs[i][:], last[:, :, a : a + P], ALU.add)
+            nc.sync.dma_start(out[:, a : a + P].rearrange("(b p) v -> p b v", p=P), res[:])
 
         centre = psum.tile([P, 2, N], F32, name="centre", tag="bank0")
-        neighbour = psum.tile([P, 2, N], F32, name="neighbour", tag="bank1")
-        pairs = [psum.tile([P, HALF], F32, name=f"pair{b}", tag=f"bank{5 + b}") for b in range(2)]
-        plain_c0 = plain(0, cen_t, "c")
+        neighbours = [psum.tile([P, N], F32, name=f"neighbour{i}", tag=f"bank{1 + 2 * i}") for i in range(2)]
+        pairs = [psum.tile([P, 2, P], F32, name=f"pair{i}", tag=f"bank{5 + i}") for i in range(2)]
+        last = keep.tile([P, 2, V], F32, name="last")
+        plain_c0 = centre_in(0)
         product(1, 0, 512, 4)
         product(1, 512, 1024, 7)
         turn_in(centre, 0, plain_c0)
-        near = [term(0, pos1_t, first[:, :HALF], HALF, "near")]
-        last = [term(0, pos2_t, second[:], V, "last")]
-        there0 = add_up(0, [near[0], last[0], term(0, cen_t, own, HALF, "self")], 2)
-        turn_in(centre, 1, plain(1, cen_t, "c"))
-        turn_in(neighbour, 0, plain(0, pos1_t, "n", "w_codes1"))
-        turn_in(neighbour, 1, plain(1, pos1_t, "n"))
-        near.append(term(1, pos1_t, first[:, :HALF], HALF, "near"))
-        last.append(term(1, pos2_t, second[:], V, "last"))
-        back0 = turn_back(0, there0)
-        scaled = [scale_centre(i) for i in range(2)]
-        here = plain(1, cen_t, "h", "plainn1", 0)
-        finish_first(0, back0)
-        for i in range(2):
-            join_back(i, scaled[i])
-        both = keep.tile([P, HALF], F32, name="both", tag="scaled0")
-        nc.vector.tensor_tensor(both[:], near[1][:], last[1][:, :HALF], ALU.add)
+        near0 = term(0, pos1_t, first[:, :HALF], "near")
+        fused(last[:, 0, :], 0, pos2_t, second[:], 0, V)
+        there0 = add_up(0, [near0, last[:, 0, :], term(0, cen_t, own, "self")], 2)
+        turn_in(centre, 1, centre_in(1))
+        plain_n0 = keep.tile([P, HALF], F32, name="plain_n0", tag="w_codes1", align_bytes=64)
+        plain_n1 = [
+            turns.tile([P, P], F32, name="plain_n1_0", offset=2 * BAND_BYTES),
+            keep.tile([P, P], F32, name="plain_n1_1", tag="plain_n1_1"),
+        ]
+        neighbour_in(plain_n0[:, :P], 0, 0)
+        neighbour_in(plain_n1[0][:], 1, 0)
+        neighbour_in(plain_n0[:, P:], 0, 1)
+        near1 = term(1, pos1_t, first[:, :HALF], "near")
+        fused(last[:, 1, :], 1, pos2_t, second[:], 0, V)
+        join_back(0, scale_centre(0))
+        neighbour_in(plain_n1[1][:], 1, 1)
+        both = turns.tile([P, HALF], F32, name="both", offset=2 * BAND_BYTES)
+        nc.vector.tensor_tensor(both[:], near1[:], last[:, 1, :HALF], ALU.add)
+        join_back(1, scale_centre(1))
+        here = keep.tile([P, HALF], F32, name="here", tag="plain_n1_1")
+        plain(here[:], 1, cen_t, 0, HALF)
+        finish_first(0, turn_back(0, there0))
         stay = keep.tile([P, HALF], F32, name="stay")
         nc.vector.tensor_tensor(stay[:], here[:], own, ALU.mult)
         finish_second(0)

@@ -23,6 +23,8 @@ QUAD = 32
 HALF = V // 2
 BLOCKS = V // P
 FIRST = P - K // 32
+GATE0 = P - 2 * BLOCKS
+GATE1 = P - BLOCKS
 CUT = 768
 BAND_BYTES = P * PACK * 2
 
@@ -44,10 +46,11 @@ def tile_picked_grand_relu_p_kernel(tc, x_words, x_scales, w1, gate, offs, cen, 
         gate_rows = keep.tile([P, P], F32, name="gate_rows")
 
         nc.vector.memset(scale_tab[:FIRST, :].bitcast(I32), 0)
+        nc.vector.memset(gate_rows[:GATE0, :], 0.0)
         nc.scalar.dma_start(scale_tab[FIRST:, :].bitcast(I32), x_scales[0].bitcast(I32))
         nc.sync.dma_start(offs_t[:], offs)
-        middle = gate.rearrange("d p v -> (d p) v")[P - LANES : P + LANES, :]
-        nc.sync.dma_start(gate_rows[:], middle.rearrange("r (b c) -> (r b) c", c=P))
+        middle = gate.rearrange("d p v -> (d p) v")[P - 1 : P + 1, :]
+        nc.sync.dma_start(gate_rows[GATE0:, :], middle.rearrange("r (b c) -> (r b) c", c=P))
         nc.sync.dma_start(word_tab[:], x_words[0].rearrange("p n t -> p (n t)").bitcast(I32))
         nc.sync.dma_start(w_raw[:], w1.rearrange("(p j) m -> p j m", j=PACK))
         nc.sync.dma_start(cen_t[:], cen)
@@ -75,13 +78,13 @@ def tile_picked_grand_relu_p_kernel(tc, x_words, x_scales, w1, gate, offs, cen, 
             turns.tile([P, 1], F32, name="own_late0", offset=2 * BAND_BYTES + P * 4),
             keep.tile([P, 1], F32, name="own_late1"),
         ]
-        nc.scalar.copy(cols1[:, :, :2], turned[:, P // 2 : P // 2 + BLOCKS].rearrange("p (a b) -> p a b", a=2))
-        nc.scalar.copy(cols0[:], turned[:, :BLOCKS])
-        nc.scalar.activation(rest[:], turned[:, :BLOCKS], ACT.Identity, bias=1.0, scale=-1.0)
+        nc.scalar.copy(cols1[:, :, :2], turned[:, GATE1:].rearrange("p (a b) -> p a b", a=2))
+        nc.scalar.copy(cols0[:], turned[:, GATE0:GATE1])
+        nc.scalar.activation(rest[:], turned[:, GATE0:GATE1], ACT.Identity, bias=1.0, scale=-1.0)
         for j in range(BLOCKS):
             own = own_early[:, j : j + 1] if j < 2 else own_late[j - 2][:]
             nc.scalar.activation(
-                own, turned[:, P // 2 + j : P // 2 + j + 1], ACT.Identity, bias=rest[:, j : j + 1], scale=-1.0
+                own, turned[:, GATE1 + j : GATE1 + j + 1], ACT.Identity, bias=rest[:, j : j + 1], scale=-1.0
             )
 
         def spread(columns, bank):
@@ -137,8 +140,8 @@ def tile_picked_grand_relu_p_kernel(tc, x_words, x_scales, w1, gate, offs, cen, 
 
         for i in range(3):
             product(0, i * 256, (i + 1) * 256, i, i == 2)
-        product(0, 768, 896, 3)
-        product(0, 896, 1024, 7, True)
+        product(0, 768, 896, 3, True)
+        product(0, 896, 1024, 7)
 
         def fused(part, b, lst, factor, v0, v1):
             nc.vector.tensor_tensor(part, y[b][:].indirect(lst[:, v0 // LANES : v1 // LANES]), factor, ALU.mult)
@@ -206,13 +209,14 @@ def tile_picked_grand_relu_p_kernel(tc, x_words, x_scales, w1, gate, offs, cen, 
             nc.vector.tensor_tensor(res[:], pairs[i][:], last[:, :, a : a + P], ALU.add)
             nc.sync.dma_start(out[:, a : a + P].rearrange("(b p) v -> p b v", p=P), res[:])
 
-        centre = psum.tile([P, 2, N], F32, name="centre", tag="bank0")
         neighbours = [psum.tile([P, N], F32, name=f"neighbour{i}", tag=f"bank{1 + 2 * i}") for i in range(2)]
         pairs = [psum.tile([P, 2, P], F32, name=f"pair{i}", tag=f"bank{5 + i}") for i in range(2)]
         last = keep.tile([P, 2, V], F32, name="last")
+        product(1, 0, 256, 4)
+        product(1, 256, 512, 0)
         plain_c0 = centre_in(0)
-        product(1, 0, 512, 4)
         product(1, 512, 1024, 7)
+        centre = psum.tile([P, 2, N], F32, name="centre", tag="bank0")
         turn_in(centre, 0, plain_c0)
         near0 = term(0, pos1_t, first[:, :HALF], "near")
         fused(last[:, 0, :], 0, pos2_t, second[:], 0, V)

@@ -62,23 +62,20 @@ def tile_picked_grand_relu_p_kernel(tc, x_words, x_scales, w1, gate, offs, cen, 
 
         picked = keep.tile([P, S], U8, name="picked", align_bytes=64)
         nc.vector.tensor_copy(picked[:], scale_tab[:].indirect(offs_t[:]))
-        x_scale = keep.tile([P, S], U8, name="x_scale", align_bytes=64)
-        for r in range(PACK):
-            nc.sync.dma_start(x_scale[r:P:QUAD, :].bitcast(I32), picked[FIRST + r : P : PACK, :].bitcast(I32))
         x_codes = [keep.tile([P, CUT], U32, name="x_codes0", align_bytes=64)]
         nc.vector.tensor_copy(x_codes[0][:], word_tab[:].bitcast(U32).indirect(offs_t[:, : CUT // LANES]))
 
         turned = psum.tile([P, P], F32, name="turned", tag="bank7")
         nc.tensor.transpose(turned[:], gate_rows[:], ident[:])
-        cols1 = turns.tile([P, 2, 8], F32, name="cols1", offset=BAND_BYTES - 32)
+        cols1 = turns.tile([P, BAND_BYTES // 4 + 16], F32, name="cols1", offset=S - 32)
         cols0 = keep.tile([P, BLOCKS], F32, name="cols0")
         rest = keep.tile([P, BLOCKS], F32, name="rest")
         own_early = keep.tile([P, 2], F32, name="own_early")
         own_late = [
-            turns.tile([P, 1], F32, name="own_late0", offset=2 * BAND_BYTES + P * 4),
+            turns.tile([P, 1], F32, name="own_late0", offset=S + 2 * BAND_BYTES + P * 4),
             keep.tile([P, 1], F32, name="own_late1"),
         ]
-        nc.scalar.copy(cols1[:, :, :2], turned[:, GATE1:].rearrange("p (a b) -> p a b", a=2))
+        nc.scalar.copy(cols1[:, :BLOCKS], turned[:, GATE1:])
         nc.scalar.copy(cols0[:], turned[:, GATE0:GATE1])
         nc.scalar.activation(rest[:], turned[:, GATE0:GATE1], ACT.Identity, bias=1.0, scale=-1.0)
         for j in range(BLOCKS):
@@ -94,12 +91,16 @@ def tile_picked_grand_relu_p_kernel(tc, x_words, x_scales, w1, gate, offs, cen, 
             return wide
 
         second = keep.tile([P, V], F32, name="second")
-        nc.scalar.copy(second[:], spread([cols1[:, j // 2, j % 2 : j % 2 + 1] for j in range(BLOCKS)], 6)[:])
+        nc.scalar.copy(second[:], spread([cols1[:, j : j + 1] for j in range(BLOCKS)], 6)[:])
+        x_scale = turns.tile([P, S], U8, name="x_scale", offset=0, align_bytes=64)
+        for r in range(PACK):
+            queue = nc.sync if r < 2 else nc.scalar
+            queue.dma_start(x_scale[r:P:QUAD, :].bitcast(I32), picked[FIRST + r : P : PACK, :].bitcast(I32))
         wide_first = spread([t[:, j : j + 1] for t in (cols0, own_early) for j in range(2)], 5)
 
         w_codes, w_scale = [], []
         for b in range(2):
-            grouped = turns.tile([P, P, PACK], BF16, name=f"grouped{b}", offset=b * BAND_BYTES, align_bytes=64)
+            grouped = turns.tile([P, P, PACK], BF16, name=f"grouped{b}", offset=S + b * BAND_BYTES, align_bytes=64)
             nc.scalar.copy(
                 grouped[:].rearrange("p (c i) j -> p c j i", i=PACK),
                 w_raw[:, :, b * P : (b + 1) * P].rearrange("p j (c i) -> p c j i", i=PACK),
@@ -110,7 +111,7 @@ def tile_picked_grand_relu_p_kernel(tc, x_words, x_scales, w1, gate, offs, cen, 
                 out=w_codes[b][:].bitcast(FP8X4), scales=w_scale[b][:], in_=grouped[:].rearrange("p m j -> p (m j)")
             )
             if b == 0:
-                x_codes.append(turns.tile([P, S - CUT], U32, name="x_codes1", offset=0, align_bytes=64))
+                x_codes.append(turns.tile([P, S - CUT], U32, name="x_codes1", offset=S, align_bytes=64))
                 nc.vector.tensor_copy(x_codes[1][:], word_tab[:].bitcast(U32).indirect(offs_t[:, CUT // LANES :]))
 
         first = keep.tile([P, V], F32, name="first", tag="w_raw")
@@ -224,7 +225,7 @@ def tile_picked_grand_relu_p_kernel(tc, x_words, x_scales, w1, gate, offs, cen, 
         turn_in(centre, 1, centre_in(1))
         plain_n0 = keep.tile([P, HALF], F32, name="plain_n0", tag="w_codes1", align_bytes=64)
         plain_n1 = [
-            turns.tile([P, P], F32, name="plain_n1_0", offset=2 * BAND_BYTES),
+            turns.tile([P, P], F32, name="plain_n1_0", offset=S + 2 * BAND_BYTES),
             keep.tile([P, P], F32, name="plain_n1_1", tag="plain_n1_1"),
         ]
         neighbour_in(plain_n0[:, :P], 0, 0)
@@ -234,7 +235,7 @@ def tile_picked_grand_relu_p_kernel(tc, x_words, x_scales, w1, gate, offs, cen, 
         fused(last[:, 1, :], 1, pos2_t, second[:], 0, V)
         join_back(0, scale_centre(0))
         neighbour_in(plain_n1[1][:], 1, 1)
-        both = turns.tile([P, HALF], F32, name="both", offset=2 * BAND_BYTES)
+        both = turns.tile([P, HALF], F32, name="both", offset=S + 2 * BAND_BYTES)
         nc.vector.tensor_tensor(both[:], near1[:], last[:, 1, :HALF], ALU.add)
         join_back(1, scale_centre(1))
         here = keep.tile([P, HALF], F32, name="here", tag="plain_n1_1")

from contextlib import ExitStack

import concourse.mybir as mybir
from concourse.masks import make_identity

K, T, S, V, N = 512, 2048, 1024, 512, 256
FLOPS = 2 * K * N * S

F32 = mybir.dt.float32
BF16 = mybir.dt.bfloat16
I32 = mybir.dt.int32
U32 = mybir.dt.uint32
U16 = mybir.dt.uint16
U8 = mybir.dt.uint8
FP8X4 = mybir.dt.float8_e4m3fn_x4
ALU = mybir.AluOpType
ACT = mybir.ActivationFunctionType

P = 128
PACK = 4
LANES = 16
QUAD = 32
HALF = V // 2
BLOCKS = V // P
FIRST = P - K // 32
GATE0 = P - 2 * BLOCKS
GATE1 = P - BLOCKS
CUT = 768
BAND_BYTES = P * PACK * 2


def tile_picked_grand_relu_p_kernel(tc, x_words, x_scales, w1, gate, offs, cen, pos1, pos2, out):
    nc = tc.nc
    with ExitStack() as ctx:
        keep = ctx.enter_context(tc.tile_pool(name="keep", bufs=1))
        turns = ctx.enter_context(tc.tile_pool(name="turns", bufs=1))
        psum = ctx.enter_context(tc.psum_pool(name="psum", bufs=1))

        offs_t = keep.tile([P, S // LANES], U16, name="offs_t")
        cen_t = keep.tile([P, V // LANES], U16, name="cen_t")
        pos1_t = keep.tile([P, V // LANES], U16, name="pos1_t")
        pos2_t = keep.tile([P, V // LANES], U16, name="pos2_t")
        scale_tab = keep.tile([P, T], U8, name="scale_tab", align_bytes=64)
        word_tab = keep.tile([P, T], I32, name="word_tab", align_bytes=64)
        w_raw = keep.tile([P, PACK, N], F32, name="w_raw", tag="w_raw")
        gate_rows = keep.tile([P, P], F32, name="gate_rows")

        nc.vector.memset(scale_tab[:FIRST, :].bitcast(I32), 0)
        nc.vector.memset(gate_rows[:GATE0, :], 0.0)
        nc.scalar.dma_start(scale_tab[FIRST:, :].bitcast(I32), x_scales[0].bitcast(I32))
        nc.sync.dma_start(offs_t[:], offs)
        middle = gate.rearrange("d p v -> (d p) v")[P - 1 : P + 1, :]
        nc.sync.dma_start(gate_rows[GATE0:, :], middle.rearrange("r (b c) -> (r b) c", c=P))
        nc.sync.dma_start(word_tab[:], x_words[0].rearrange("p n t -> p (n t)").bitcast(I32))
        nc.sync.dma_start(w_raw[:], w1.rearrange("(p j) m -> p j m", j=PACK))
        nc.sync.dma_start(cen_t[:], cen)
        nc.sync.dma_start(pos1_t[:], pos1)
        nc.sync.dma_start(pos2_t[:], pos2)

        ident = keep.tile([P, P], F32, name="ident")
        make_identity(nc, ident[:])

        picked = keep.tile([P, S], U8, name="picked", align_bytes=64)
        nc.vector.tensor_copy(picked[:], scale_tab[:].indirect(offs_t[:]))
        x_codes = [keep.tile([P, CUT], U32, name="x_codes0", align_bytes=64)]
        nc.vector.tensor_copy(x_codes[0][:], word_tab[:].bitcast(U32).indirect(offs_t[:, : CUT // LANES]))

        turned = psum.tile([P, P], F32, name="turned", tag="bank7")
        nc.tensor.transpose(turned[:], gate_rows[:], ident[:])
        cols1 = turns.tile([P, BAND_BYTES // 4 + 16], F32, name="cols1", offset=S - 32)
        cols0 = keep.tile([P, BLOCKS], F32, name="cols0")
        rest = keep.tile([P, BLOCKS], F32, name="rest")
        own_early = keep.tile([P, 2], F32, name="own_early")
        own_late = [
            turns.tile([P, 1], F32, name="own_late0", offset=S + 2 * BAND_BYTES + P * 4),
            keep.tile([P, 1], F32, name="own_late1"),
        ]
        nc.scalar.copy(cols1[:, :BLOCKS], turned[:, GATE1:])
        nc.scalar.copy(cols0[:], turned[:, GATE0:GATE1])
        nc.scalar.activation(rest[:], turned[:, GATE0:GATE1], ACT.Identity, bias=1.0, scale=-1.0)
        for j in range(BLOCKS):
            own = own_early[:, j : j + 1] if j < 2 else own_late[j - 2][:]
            nc.scalar.activation(
                own, turned[:, GATE1 + j : GATE1 + j + 1], ACT.Identity, bias=rest[:, j : j + 1], scale=-1.0
            )

        def spread(columns, bank):
            wide = psum.tile([P, V], F32, name=f"wide{bank}", tag=f"bank{bank}")
            for i, column in enumerate(columns):
                nc.tensor.transpose(wide[:, i * P : (i + 1) * P], column.to_broadcast([P, P]), ident[:])
            return wide

        second = keep.tile([P, V], F32, name="second")
        nc.scalar.copy(second[:], spread([cols1[:, j : j + 1] for j in range(BLOCKS)], 6)[:])
        x_scale = turns.tile([P, S], U8, name="x_scale", offset=0, align_bytes=64)
        for r in range(PACK):
            queue = nc.sync if r < 2 else nc.scalar
            queue.dma_start(x_scale[r:P:QUAD, :].bitcast(I32), picked[FIRST + r : P : PACK, :].bitcast(I32))
        wide_first = spread([t[:, j : j + 1] for t in (cols0, own_early) for j in range(2)], 5)

        w_codes, w_scale = [], []
        for b in range(2):
            grouped = turns.tile([P, P, PACK], BF16, name=f"grouped{b}", offset=S + b * BAND_BYTES, align_bytes=64)
            nc.scalar.copy(
                grouped[:].rearrange("p (c i) j -> p c j i", i=PACK),
                w_raw[:, :, b * P : (b + 1) * P].rearrange("p j (c i) -> p c j i", i=PACK),
            )
            w_codes.append(keep.tile([P, P], U32, name=f"w_codes{b}", tag=f"w_codes{b}", align_bytes=64))
            w_scale.append(keep.tile([P, P], U8, name=f"w_scale{b}", align_bytes=64))
            nc.vector.quantize_mx(
                out=w_codes[b][:].bitcast(FP8X4), scales=w_scale[b][:], in_=grouped[:].rearrange("p m j -> p (m j)")
            )
            if b == 0:
                x_codes.append(turns.tile([P, S - CUT], U32, name="x_codes1", offset=S, align_bytes=64))
                nc.vector.tensor_copy(x_codes[1][:], word_tab[:].bitcast(U32).indirect(offs_t[:, CUT // LANES :]))

        first = keep.tile([P, V], F32, name="first", tag="w_raw")
        nc.scalar.copy(first[:], wide_first[:])
        own = first[:, HALF:]
        y = [keep.tile([P, S], F32, name=f"y{b}") for b in range(2)]

        def product(b, a0, z0, bank, on_vector=False):
            acc = psum.tile([P, z0 - a0], F32, name=f"acc{b}_{a0}", tag=f"bank{bank}")
            for a, z in ((a0, CUT), (CUT, z0)) if a0 < CUT < z0 else ((a0, z0),):
                one_pass(acc[:, a - a0 : z - a0], b, a, z)
            if on_vector:
                nc.vector.tensor_scalar_max(y[b][:, a0:z0], acc[:], 0.0)
            else:
                nc.scalar.activation(y[b][:, a0:z0], acc[:], ACT.Relu)

        def one_pass(acc, b, a, z):
            nc.tensor.matmul_mx(
                out=acc,
                lhsT=w_codes[b][:].bitcast(FP8X4),
                lhsT_scale=w_scale[b][:],
                rhs=x_codes[a // CUT][:, a % CUT : a % CUT + z - a].bitcast(FP8X4),
                rhs_scale=x_scale[:, a:z],
                start=True,
                stop=True,
            )

        for i in range(3):
            product(0, i * 256, (i + 1) * 256, i, i == 2)
        product(0, 768, 896, 3, True)
        product(0, 896, 1024, 7)

        def fused(part, b, lst, factor, v0, v1):
            nc.vector.tensor_tensor(part, y[b][:].indirect(lst[:, v0 // LANES : v1 // LANES]), factor, ALU.mult)

        def plain(part, b, lst, v0, v1):
            nc.scalar.activation(part, y[b][:].indirect(lst[:, v0 // LANES : v1 // LANES]), ACT.Copy)

        def centre_in(b):
            part = keep.tile([P, HALF], F32, name=f"plain_centre{b}")
            plain(part[:], b, cen_t, HALF, V)
            return part

        def neighbour_in(part, b, i):
            plain(part, b, pos1_t, HALF + i * P, HALF + (i + 1) * P)
            nc.tensor.transpose(neighbours[i][:, b * P : (b + 1) * P], part, ident[:])

        def turn(acc, part, start, stop):
            nc.tensor.matmul(acc, part, ident[:], start=start, stop=stop, is_transpose=True)

        def term(b, lst, factor, name):
            part = keep.tile([P, HALF], F32, name=f"{name}{b}")
            fused(part[:], b, lst, factor, 0, HALF)
            return part

        def add_up(b, parts, bank):
            there = psum.tile([P, 2, P], F32, name=f"there{b}", tag=f"bank{bank}")
            for t, part in enumerate(parts):
                for i in range(2):
                    turn(there[:, i, :], part[:, i * P : (i + 1) * P], (t, i) == (0, 0), (t, i) == (2, 1))
            return there

        def turn_back(b, there):
            summed = keep.tile([P, 2, P], F32, name=f"summed{b}")
            nc.scalar.copy(summed[:], there[:])
            back = psum.tile([P, HALF], F32, name=f"back{b}", tag=f"bank{(7, 4)[b]}")
            for i in range(2):
                nc.tensor.transpose(back[:, i * P : (i + 1) * P], summed[:, i, :], ident[:])
            return back

        def turn_in(there, b, part):
            for i in range(2):
                nc.tensor.transpose(there[:, i, b * P : (b + 1) * P], part[:, i * P : (i + 1) * P], ident[:])

        def scale_centre(i):
            scaled = keep.tile([P, N], F32, name=f"scaled{i}", tag=f"scaled{i}")
            nc.scalar.activation(scaled[:], centre[:, i, :], ACT.Copy, scale=own_late[i][:])
            return scaled

        def join_back(i, scaled):
            joined = keep.tile([P, N], F32, name=f"joined{i}")
            nc.vector.scalar_tensor_tensor(
                joined[:], neighbours[i][:], cols0[:, 2 + i : 3 + i], scaled[:], ALU.mult, ALU.add
            )
            for b in range(2):
                nc.tensor.transpose(pairs[i][:, b, :], joined[:, b * P : (b + 1) * P], ident[:])

        def finish_first(b, back):
            res = keep.tile([P, HALF], F32, name=f"res{b}")
            nc.scalar.copy(res[:], back[:])
            nc.scalar.dma_start(out[b * P : (b + 1) * P, :HALF], res[:])

        def finish_second(i):
            a = HALF + i * P
            res = keep.tile([P, 2, P], F32, name=f"end{i}")
            nc.vector.tensor_tensor(res[:], pairs[i][:], last[:, :, a : a + P], ALU.add)
            nc.sync.dma_start(out[:, a : a + P].rearrange("(b p) v -> p b v", p=P), res[:])

        neighbours = [psum.tile([P, N], F32, name=f"neighbour{i}", tag=f"bank{1 + 2 * i}") for i in range(2)]
        pairs = [psum.tile([P, 2, P], F32, name=f"pair{i}", tag=f"bank{5 + i}") for i in range(2)]
        last = keep.tile([P, 2, V], F32, name="last")
        product(1, 0, 256, 4)
        product(1, 256, 512, 0)
        plain_c0 = centre_in(0)
        product(1, 512, 1024, 7)
        centre = psum.tile([P, 2, N], F32, name="centre", tag="bank0")
        turn_in(centre, 0, plain_c0)
        near0 = term(0, pos1_t, first[:, :HALF], "near")
        fused(last[:, 0, :], 0, pos2_t, second[:], 0, V)
        there0 = add_up(0, [near0, last[:, 0, :], term(0, cen_t, own, "self")], 2)
        turn_in(centre, 1, centre_in(1))
        plain_n0 = keep.tile([P, HALF], F32, name="plain_n0", tag="w_codes1", align_bytes=64)
        plain_n1 = [
            turns.tile([P, P], F32, name="plain_n1_0", offset=S + 2 * BAND_BYTES),
            keep.tile([P, P], F32, name="plain_n1_1", tag="plain_n1_1"),
        ]
        neighbour_in(plain_n0[:, :P], 0, 0)
        neighbour_in(plain_n1[0][:], 1, 0)
        neighbour_in(plain_n0[:, P:], 0, 1)
        near1 = term(1, pos1_t, first[:, :HALF], "near")
        fused(last[:, 1, :], 1, pos2_t, second[:], 0, V)
        join_back(0, scale_centre(0))
        neighbour_in(plain_n1[1][:], 1, 1)
        both = turns.tile([P, HALF], F32, name="both", offset=S + 2 * BAND_BYTES)
        nc.vector.tensor_tensor(both[:], near1[:], last[:, 1, :HALF], ALU.add)
        join_back(1, scale_centre(1))
        here = keep.tile([P, HALF], F32, name="here", tag="plain_n1_1")
        plain(here[:], 1, cen_t, 0, HALF)
        finish_first(0, turn_back(0, there0))
        stay = keep.tile([P, HALF], F32, name="stay")
        nc.vector.tensor_tensor(stay[:], here[:], own, ALU.mult)
        finish_second(0)
        res = keep.tile([P, HALF], F32, name="res1")
        nc.vector.tensor_tensor(res[:], stay[:], both[:], ALU.add)
        nc.sync.dma_start(out[P:, :HALF], res[:])
        finish_second(1)
